import numpy as np
import ml_dtypes


def mxq(x, axis, fmt="e4m3"):
    dtype, down = {"e4m3": (ml_dtypes.float8_e4m3fn, 7), "e5m2": (ml_dtypes.float8_e5m2, 14)}[fmt]
    v = np.moveaxis(np.asarray(x, np.float32).astype(ml_dtypes.bfloat16).astype(np.float64), axis, -1)
    blocks = v.reshape(v.shape[:-1] + (-1, 32))
    amax = np.abs(blocks).max(-1, keepdims=True)
    byte = np.maximum(np.where(amax > 0, np.frexp(amax)[1] - 1 + 127, 0) - down, 1)
    scale = np.exp2(byte - 127.0)
    codes = (blocks / scale).astype(np.float32).astype(dtype).astype(np.float64)
    return np.moveaxis((codes * scale).reshape(v.shape), -1, axis)


WIDE = False


def mx_kscale(k):
    if not WIDE:
        return np.ones(k)
    levels = np.array([10, -10, 5, -5, 0])
    if k % 512:
        return np.exp2(np.random.permutation(np.resize(levels, k // 32))).repeat(32)
    a = np.empty((k // 512, 16))
    for p in range(k // 512):
        a[p, :8] = np.random.permutation(np.resize(levels, 8))
        for g in range(8):
            far = levels[np.abs(levels - a[p, g]) >= 10]
            a[p, g + 8] = far[np.random.randint(len(far))]
    return np.exp2(a.ravel()).repeat(32)


def f64(x):
    return np.asarray(x).astype(np.float64)


E2M1 = np.array([0.0, 0.5, 1.0, 1.5, 2.0, 3.0, 4.0, 6.0, -0.0, -0.5, -1.0, -1.5, -2.0, -3.0, -4.0, -6.0])


def pack_weight(w, fmt):
    k, n = w.shape
    w = f64(np.asarray(w, np.float32).astype(ml_dtypes.bfloat16)).reshape(k // 32, 32, n)
    amax = np.abs(w).max(1)
    if fmt == "e4m3":
        byte = np.frexp(amax)[1] - 1 + 127 - 7
    else:
        mant, ex = np.frexp(amax / 6.0)
        byte = np.where(mant > 0.5, ex, ex - 1) + 127
    byte = np.clip(np.where(amax > 0, byte, 1), 1, 254)
    scaled = (w * np.exp2(127.0 - byte)[:, None, :]).reshape(k, n).astype(np.float32)
    by_word = np.ascontiguousarray(scaled.reshape(k // 512, 128, 4, n).transpose(0, 1, 3, 2))
    if fmt == "e4m3":
        words = by_word.astype(ml_dtypes.float8_e4m3fn).view(np.uint8)
    else:
        c = by_word.astype(ml_dtypes.float4_e2m1fn).view(np.uint8) & 0xF
        words = (c[..., 0::2] | (c[..., 1::2] << 4)).reshape(k // 512, 128, 2 * n)
    return np.ascontiguousarray(words), np.ascontiguousarray(byte.astype(np.uint8).reshape(k // 512, 16, n))


def unpack_weight(words, scales, fmt):
    g, _, n = scales.shape
    words = np.ascontiguousarray(words).reshape(g, 128, n, -1)
    if fmt == "e4m3":
        vals = words.view(ml_dtypes.float8_e4m3fn).astype(np.float64)
    else:
        nib = np.empty((g, 128, n, 4), np.uint8)
        nib[..., 0::2] = words & 0xF
        nib[..., 1::2] = words >> 4
        vals = E2M1[nib]
    vals = vals * np.repeat(np.exp2(scales.astype(np.float64) - 127.0), 8, axis=1)[..., None]
    return vals.transpose(0, 1, 3, 2).reshape(g * 512, n)


def planes(y):
    n, m = y.shape
    v = y.astype(np.float32).astype(ml_dtypes.bfloat16).astype(np.float64).reshape(n // 32, 32, m)
    top = np.abs(v).max(1)
    byte = np.clip(np.where(top > 0, np.frexp(top)[1] - 1 + 127 - 7, 1), 1, 254)
    codes = (v * np.exp2(127.0 - byte)[:, None, :]).reshape(n, m).astype(np.float32).astype(ml_dtypes.float8_e4m3fn).view(np.uint8)
    words = codes.reshape(n // 512, 128, 4, m).transpose(0, 1, 3, 2)
    return np.ascontiguousarray(words), np.ascontiguousarray(byte.astype(np.uint8).reshape(n // 512, 16, m))


def gelu(v):
    return 0.5 * v * (1.0 + np.tanh(np.sqrt(2.0 / np.pi) * (v + 0.044715 * v**3)))


K, M, T = 2048, 1024, 512


def setup_inputs():
    n = np.random.standard_normal
    s = mx_kscale(K)[:, None]
    p_w4 = pack_weight(n((K, M)) / np.sqrt(K) / s, "e2m1")
    p_w8 = pack_weight(n((K, M)) / np.sqrt(K) / s, "e4m3")
    return {
        "x": (n((K, T)) * s).astype(np.float32),
        "w4_words": p_w4[0],
        "w4_scales": p_w4[1],
        "w8_words": p_w8[0],
        "w8_scales": p_w8[1],
        "b": (0.3 * n(1024)).astype(np.float32),
    }


def reference(x, w4_words, w4_scales, w8_words, w8_scales, b):
    xa_, xb_ = mxq(np.maximum(f64(x), 0.0), 0, "e4m3"), mxq(np.maximum(-f64(x), 0.0), 0, "e4m3")
    w4_ = unpack_weight(w4_words, w4_scales, "e2m1")
    w8_ = unpack_weight(w8_words, w8_scales, "e4m3")
    y = w4_.T @ xa_ + w8_.T @ xb_
    out_0 = gelu(y + f64(b)[:, None])
    return (out_0,) + planes(out_0)

@@ -1,0 +1,318 @@
+from contextlib import ExitStack
+
+import concourse.mybir as mybir
+from concourse.masks import make_identity
+
+K, M, T = 2048, 1024, 512
+FLOPS = 2 * 2 * K * M * T
+
+F32 = mybir.dt.float32
+BF16 = mybir.dt.bfloat16
+I32 = mybir.dt.int32
+U32 = mybir.dt.uint32
+U8 = mybir.dt.uint8
+FP8X4 = mybir.dt.float8_e4m3fn_x4
+FP4X4 = mybir.dt.float4_e2m1fn_x4
+ACT = mybir.ActivationFunctionType
+ALU = mybir.AluOpType
+
+P = 128
+PACK = 4
+K_PASS = P * PACK
+PASSES = K // K_PASS
+T_TILE = 128
+T_TILES = T // T_TILE
+N_HALF = 512
+HALVES = M // N_HALF
+QUADS = 4
+PAIR = 2
+
+
+def tile_mix_feat_fm_crelupl_gelu_kernel(
+    tc, x, w4_words, w4_scales, w8_words, w8_scales, b, out_0, out_1, out_2
+):
+    nc = tc.nc
+    last = PASSES - 1
+
+    with ExitStack() as ctx:
+        sb = ctx.enter_context(tc.tile_pool(name="sb", bufs=1))
+        psum = ctx.enter_context(tc.psum_pool(name="psum", bufs=1))
+        ctx.enter_context(tc.manual_schedule())
+
+        s4_first = sb.tile([P, M], U8, name="s4_first", align_bytes=64)
+        s4_rest = sb.tile([P, last, M], U8, name="s4_rest", align_bytes=64)
+        s8 = sb.tile([P, M], U8, name="s8", align_bytes=64)
+        nc.vector.memset(s4_first[:].bitcast(I32), 0)
+        nc.vector.memset(s8[:].bitcast(I32), 0)
+        nc.vector.memset(s4_rest[:].bitcast(I32), 0)
+
+        ident = sb.tile([P, P], F32, name="ident")
+        make_identity(nc, ident[:])
+
+        preload = sb.tile([P, 1], F32, name="preload")
+        nc.scalar.activation(out=preload[:], in_=ident[:, 0:1], func=ACT.Gelu_apprx_tanh)
+
+        s4_rows = w4_scales.bitcast(I32).rearrange("a (g r) n -> r g a n", r=QUADS)
+        s8_rows = w8_scales.bitcast(I32)
+        w8_rows = w8_words.rearrange("a p n i -> a p (n i)").bitcast(I32)
+        raw = {}
+        w4 = {}
+        w8 = {}
+
+        def load_x(a):
+            raw[a] = sb.tile([P, PACK, T], F32, name="raw%d" % a)
+            rows = x[a * K_PASS : (a + 1) * K_PASS, :]
+            nc.sync.dma_start(out=raw[a][:], in_=rows.rearrange("(p j) t -> p j t", j=PACK))
+
+        def load_w4(a):
+            w4[a] = sb.tile([P, 2 * M], U8, name="w4_%d" % a, align_bytes=64)
+            nc.sync.dma_start(out=w4[a][:].bitcast(I32), in_=w4_words[a].bitcast(I32))
+
+        def load_w8(a, halves):
+            width = N_HALF * len(halves)
+            n0 = N_HALF * halves[0]
+            words = sb.tile([P, width], U32, name="w8_%d_%d" % (a, halves[0]), align_bytes=64)
+            nc.sync.dma_start(out=words[:].bitcast(I32), in_=w8_rows[a, :, n0 : n0 + width])
+            for h in halves:
+                w8[a, h] = words[:, N_HALF * h - n0 : N_HALF * (h + 1) - n0]
+
+        load_x(0)
+        for r in range(QUADS):
+            nc.sync.dma_start(out=s4_first[:].bitcast(I32)[r:P:32, :], in_=s4_rows[r, :, 0, :])
+        load_w4(0)
+        for g in range(QUADS):
+            nc.sync.dma_start(
+                out=s8[:].bitcast(I32)[32 * g : 32 * g + 16, :], in_=s8_rows[:, 4 * g : 4 * g + 4, :]
+            )
+        load_w8(0, [0, 1])
+        for r in range(QUADS):
+            nc.sync.dma_start(out=s4_rest[:].bitcast(I32)[r:P:32, :, :], in_=s4_rows[r, :, 1:PASSES, :])
+        for a in range(1, last):
+            load_x(a)
+            load_w4(a)
+            load_w8(a, [0, 1])
+        load_x(last)
+        load_w4(last)
+        load_w8(last, [0])
+        load_w8(last, [1])
+        bias = sb.tile([P, HALVES, PACK], F32, name="bias")
+        nc.sync.dma_start(out=bias[:], in_=b.rearrange("(h p r) -> p h r", h=HALVES, r=PACK))
+
+        rounded = {}
+        codes = {}
+        scales = {}
+
+        def grouped(tile_ap):
+            return tile_ap.rearrange("p (c i j) -> p c j i", i=PAIR, j=PACK)
+
+        def by_pairs(rows_ap):
+            return rows_ap.rearrange("p j (c i) -> p c j i", i=PAIR)
+
+        def positive_part(a, tt):
+            dst = sb.tile([P, PACK * T_TILE], BF16, name="xa%d_%d" % (a, tt), align_bytes=64)
+            nc.vector.tensor_scalar(
+                out=grouped(dst[:]),
+                in0=by_pairs(raw[a][:, :, tt * T_TILE : (tt + 1) * T_TILE]),
+                scalar1=0.0,
+                scalar2=None,
+                op0=ALU.max,
+            )
+            rounded["a", a, tt] = dst
+
+        def negative_part(a, tt):
+            dst = sb.tile([P, PACK * T_TILE], BF16, name="xb%d_%d" % (a, tt), align_bytes=64)
+            nc.scalar.activation(
+                out=grouped(dst[:]),
+                in_=by_pairs(raw[a][:, :, tt * T_TILE : (tt + 1) * T_TILE]),
+                func=ACT.Relu,
+                scale=-1.0,
+            )
+            rounded["b", a, tt] = dst
+
+        def quantize_x(part, a, tt):
+            key = (part, a, tt)
+            codes[key] = sb.tile([P, T_TILE], U32, name="c%s%d_%d" % key, align_bytes=64)
+            scales[key] = sb.tile([P, T_TILE], U8, name="s%s%d_%d" % key, align_bytes=64)
+            nc.vector.quantize_mx(out=codes[key][:].bitcast(FP8X4), scales=scales[key][:], in_=rounded[key][:])
+
+        groups = [(h, tt) for h in range(HALVES) for tt in range(T_TILES)]
+        acc = []
+        for g in range(len(groups)):
+            acc.append(psum.tile([P, N_HALF], F32, name="acc%d" % g, tag="bank%d" % g))
+
+        def product_w4(a, g):
+            h, tt = groups[g]
+            plane = s4_first[:, :] if a == 0 else s4_rest[:, a - 1, :]
+            nc.tensor.matmul_mx(
+                out=acc[g][:],
+                lhsT=codes["a", a, tt][:].bitcast(FP8X4),
+                lhsT_scale=scales["a", a, tt][:],
+                rhs=w4[a][:, 2 * N_HALF * h : 2 * N_HALF * (h + 1)].bitcast(FP4X4),
+                rhs_scale=plane[:, N_HALF * h : N_HALF * (h + 1)],
+                start=(a == 0),
+                stop=False,
+            )
+
+        def product_w8(a, g):
+            h, tt = groups[g]
+            nc.tensor.matmul_mx(
+                out=acc[g][:],
+                lhsT=codes["b", a, tt][:].bitcast(FP8X4),
+                lhsT_scale=scales["b", a, tt][:],
+                rhs=w8[a, h].bitcast(FP8X4),
+                rhs_scale=s8[4 * a : P, N_HALF * h : N_HALF * (h + 1)],
+                start=False,
+                stop=(a == last),
+            )
+
+        by_token_tile = [h * T_TILES + tt for tt in range(T_TILES) for h in range(HALVES)]
+        for a in range(last):
+            for tt in range(T_TILES):
+                negative_part(a, tt)
+            positive_part(a, 0)
+            for tt in range(1, T_TILES):
+                positive_part(a, tt)
+                quantize_x("a", a, tt - 1)
+            quantize_x("b", a, 0)
+            quantize_x("a", a, T_TILES - 1)
+            for tt in range(1, T_TILES):
+                quantize_x("b", a, tt)
+            for g in by_token_tile:
+                product_w4(a, g)
+            for g in by_token_tile:
+                product_w8(a, g)
+
+        for tt in range(T_TILES):
+            negative_part(last, tt)
+        positive_part(last, 0)
+        for tt in range(T_TILES):
+            if tt + 1 < T_TILES:
+                positive_part(last, tt + 1)
+            quantize_x("a", last, tt)
+            quantize_x("b", last, tt)
+
+        dealt = {}
+        turned = {}
+        result = {}
+        narrow = {}
+        out_codes = {}
+        out_scales = sb.tile([P, M], U8, name="out_scales", align_bytes=64)
+
+        def finish(g):
+            product_w4(last, g)
+            product_w8(last, g)
+
+        def deal(g, on_vector):
+            dealt[g] = sb.tile([P, PACK, P], F32, name="dealt%d" % g)
+            src = acc[g][:].rearrange("t (p r) -> t r p", r=PACK)
+            if on_vector:
+                nc.vector.tensor_copy(out=dealt[g][:], in_=src)
+            else:
+                nc.scalar.copy(out=dealt[g][:], in_=src)
+
+        def turn(unit):
+            per_bank = PACK // len(unit)
+            width = T_TILE * len(unit)
+            for i, g in enumerate(unit):
+                bank = psum.tile([P, per_bank, width], F32, name="turned%d" % g, tag="bank%d" % g)
+                for rr in range(per_bank):
+                    r = i * per_bank + rr
+                    turned[unit, r] = bank[:, rr, :]
+                    for j, src in enumerate(unit):
+                        nc.tensor.transpose(
+                            bank[:, rr, j * T_TILE : (j + 1) * T_TILE], dealt[src][:, r, :], ident[:]
+                        )
+
+        def columns(unit):
+            h, tt = groups[unit[0]]
+            return h, tt * T_TILE, T_TILE * len(unit)
+
+        def gelu(unit):
+            h, t0, width = columns(unit)
+            result[unit] = sb.tile([P, PACK, width], F32, name="result%d" % unit[0])
+            for r in range(PACK):
+                nc.scalar.activation(
+                    out=result[unit][:, r, :],
+                    in_=turned[unit, r],
+                    func=ACT.Gelu_apprx_tanh,
+                    bias=bias[:, h, r : r + 1],
+                )
+
+        def store_result(unit):
+            h, t0, width = columns(unit)
+            rows = out_0[N_HALF * h : N_HALF * (h + 1), t0 : t0 + width]
+            nc.sync.dma_start(out=rows.rearrange("(p r) t -> p r t", r=PACK), in_=result[unit][:])
+
+        def round_result(unit):
+            h, t0, width = columns(unit)
+            narrow[unit] = sb.tile([P, PACK * width], BF16, name="narrow%d" % unit[0], align_bytes=64)
+            nc.vector.tensor_copy(out=grouped(narrow[unit][:]), in_=by_pairs(result[unit][:]))
+
+        def quantize_result(unit):
+            h, t0, width = columns(unit)
+            pair = (h, t0 // (2 * T_TILE))
+            if pair not in out_codes:
+                out_codes[pair] = sb.tile([P, 2 * T_TILE], U32, name="out_codes%d_%d" % pair, align_bytes=64)
+            c0 = t0 - pair[1] * 2 * T_TILE
+            nc.vector.quantize_mx(
+                out=out_codes[pair][:, c0 : c0 + width].bitcast(FP8X4),
+                scales=out_scales[:, T * h + t0 : T * h + t0 + width],
+                in_=narrow[unit][:],
+            )
+
+        code_rows = out_1.rearrange("a p t i -> a p (t i)").bitcast(I32)
+
+        def store_codes(pair):
+            h, half = pair
+            t0 = half * 2 * T_TILE
+            nc.sync.dma_start(out=code_rows[h, :, t0 : t0 + 2 * T_TILE], in_=out_codes[pair][:].bitcast(I32))
+
+        u01, u23, u45, u6, u7 = (0, 1), (2, 3), (4, 5), (6,), (7,)
+        for g in range(4):
+            finish(g)
+        deal(0, True)
+        deal(1, False)
+        deal(2, True)
+        deal(3, False)
+        turn(u01)
+        turn(u23)
+        gelu(u01)
+        store_result(u01)
+        finish(4)
+        finish(5)
+        finish(6)
+        deal(4, True)
+        deal(5, True)
+        gelu(u23)
+        store_result(u23)
+        deal(6, False)
+        turn(u45)
+        finish(7)
+        round_result(u01)
+        round_result(u23)
+        quantize_result(u01)
+        store_codes((0, 0))
+        deal(7, True)
+        turn(u6)
+        turn(u7)
+        gelu(u45)
+        store_result(u45)
+        quantize_result(u23)
+        store_codes((0, 1))
+        gelu(u6)
+        store_result(u6)
+        gelu(u7)
+        store_result(u7)
+        round_result(u45)
+        round_result(u6)
+        quantize_result(u45)
+        store_codes((1, 0))
+        round_result(u7)
+        quantize_result(u6)
+        quantize_result(u7)
+        store_codes((1, 1))
+        scale_rows = out_2.bitcast(I32).rearrange("a (g r) t -> r g a t", r=QUADS)
+        planes = out_scales[:].bitcast(I32).rearrange("p (a t) -> p a t", a=HALVES)
+        for r in range(QUADS):
+            queue = nc.sync if r % 2 == 0 else nc.scalar
+            queue.dma_start(out=scale_rows[r], in_=planes[r:P:32, :, :])

@@ -26,6 +26,7 @@ N_HALF = 512
 HALVES = M // N_HALF
 QUADS = 4
 PAIR = 2
+WARM_UP_PASSES = 32
 
 
 def tile_mix_feat_fm_crelupl_gelu_kernel(
@@ -42,19 +43,32 @@ def tile_mix_feat_fm_crelupl_gelu_kernel(
         s4_first = sb.tile([P, M], U8, name="s4_first", align_bytes=64)
         s4_rest = sb.tile([P, last, M], U8, name="s4_rest", align_bytes=64)
         s8 = sb.tile([P, M], U8, name="s8", align_bytes=64)
+        ones = sb.tile([P, PACK * P], BF16, name="ones", align_bytes=64)
+        warm_codes = sb.tile([P, P], U32, name="warm_codes", align_bytes=64)
+        warm_scales = sb.tile([P, P], U8, name="warm_scales", align_bytes=64)
+        nc.vector.memset(ones[:], 1.0)
         nc.vector.memset(s4_first[:].bitcast(I32), 0)
+        nc.vector.quantize_mx(out=warm_codes[:].bitcast(FP8X4), scales=warm_scales[:], in_=ones[:])
         nc.vector.memset(s8[:].bitcast(I32), 0)
         nc.vector.memset(s4_rest[:].bitcast(I32), 0)
-
         ident = sb.tile([P, P], F32, name="ident")
         make_identity(nc, ident[:])
-
-        preload = sb.tile([P, 1], F32, name="preload")
-        nc.scalar.activation(out=preload[:], in_=ident[:, 0:1], func=ACT.Gelu_apprx_tanh)
+        warm = psum.tile([P, P], F32, name="warm", tag="bank7")
+        for i in range(WARM_UP_PASSES):
+            nc.tensor.matmul_mx(
+                out=warm[:],
+                lhsT=warm_codes[:].bitcast(FP8X4),
+                lhsT_scale=warm_scales[:],
+                rhs=warm_codes[:].bitcast(FP8X4),
+                rhs_scale=warm_scales[:],
+                start=True,
+                stop=True,
+            )
 
         s4_rows = w4_scales.bitcast(I32).rearrange("a (g r) n -> r g a n", r=QUADS)
         s8_rows = w8_scales.bitcast(I32)
-        w8_rows = w8_words.rearrange("a p n i -> a p (n i)").bitcast(I32)
+        w4_rows = w4_words.bitcast(I32).rearrange("a p n -> p a n")
+        w8_rows = w8_words.rearrange("a p n i -> p a (n i)").bitcast(I32)
         raw = {}
         w4 = {}
         w8 = {}
@@ -64,37 +78,50 @@ def tile_mix_feat_fm_crelupl_gelu_kernel(
             rows = x[a * K_PASS : (a + 1) * K_PASS, :]
             nc.sync.dma_start(out=raw[a][:], in_=rows.rearrange("(p j) t -> p j t", j=PACK))
 
-        def load_w4(a):
-            w4[a] = sb.tile([P, 2 * M], U8, name="w4_%d" % a, align_bytes=64)
-            nc.sync.dma_start(out=w4[a][:].bitcast(I32), in_=w4_words[a].bitcast(I32))
+        def load_w4(passes, halves):
+            n0, n1 = N_HALF * halves[0], N_HALF * (halves[-1] + 1)
+            name = "w4_%d_%d" % (passes[0], halves[0])
+            words = sb.tile([P, len(passes), 2 * (n1 - n0)], U8, name=name, align_bytes=64)
+            src = w4_rows[:, passes[0] : passes[-1] + 1, n0 // 2 : n1 // 2]
+            nc.sync.dma_start(out=words[:].bitcast(I32), in_=src)
+            for i, a in enumerate(passes):
+                for h in halves:
+                    w4[a, h] = words[:, i, 2 * (N_HALF * h - n0) : 2 * (N_HALF * (h + 1) - n0)]
 
-        def load_w8(a, halves):
-            width = N_HALF * len(halves)
-            n0 = N_HALF * halves[0]
-            words = sb.tile([P, width], U32, name="w8_%d_%d" % (a, halves[0]), align_bytes=64)
-            nc.sync.dma_start(out=words[:].bitcast(I32), in_=w8_rows[a, :, n0 : n0 + width])
-            for h in halves:
-                w8[a, h] = words[:, N_HALF * h - n0 : N_HALF * (h + 1) - n0]
+        def load_w8(passes, halves):
+            n0, n1 = N_HALF * halves[0], N_HALF * (halves[-1] + 1)
+            name = "w8_%d_%d" % (passes[0], halves[0])
+            words = sb.tile([P, len(passes), n1 - n0], U32, name=name, align_bytes=64)
+            src = w8_rows[:, passes[0] : passes[-1] + 1, n0:n1]
+            nc.sync.dma_start(out=words[:].bitcast(I32), in_=src)
+            for i, a in enumerate(passes):
+                for h in halves:
+                    w8[a, h] = words[:, i, N_HALF * h - n0 : N_HALF * (h + 1) - n0]
 
-        load_x(0)
         for r in range(QUADS):
-            nc.sync.dma_start(out=s4_first[:].bitcast(I32)[r:P:32, :], in_=s4_rows[r, :, 0, :])
-        load_w4(0)
+            nc.scalar.dma_start(out=s4_first[:].bitcast(I32)[r:P:32, :], in_=s4_rows[r, :, 0, :])
+        load_x(0)
+        load_w4([0], [0, 1])
+        preload = sb.tile([P, 1], F32, name="preload")
+        nc.scalar.activation(out=preload[:], in_=ones[:, 0:1], func=ACT.Gelu_apprx_tanh)
         for g in range(QUADS):
-            nc.sync.dma_start(
+            nc.scalar.dma_start(
                 out=s8[:].bitcast(I32)[32 * g : 32 * g + 16, :], in_=s8_rows[:, 4 * g : 4 * g + 4, :]
             )
-        load_w8(0, [0, 1])
+        load_w8([0], [0, 1])
+        load_x(1)
         for r in range(QUADS):
             nc.sync.dma_start(out=s4_rest[:].bitcast(I32)[r:P:32, :, :], in_=s4_rows[r, :, 1:PASSES, :])
-        for a in range(1, last):
-            load_x(a)
-            load_w4(a)
-            load_w8(a, [0, 1])
-        load_x(last)
-        load_w4(last)
-        load_w8(last, [0])
-        load_w8(last, [1])
+        load_w4([1], [0, 1])
+        load_w8([1], [0, 1])
+        load_x(2)
+        load_w4([2], [0, 1])
+        load_w8([2], [0])
+        load_x(3)
+        load_w4([3], [0])
+        load_w8([3], [0])
+        load_w8([2, 3], [1])
+        load_w4([3], [1])
         bias = sb.tile([P, HALVES, PACK], F32, name="bias")
         nc.sync.dma_start(out=bias[:], in_=b.rearrange("(h p r) -> p h r", h=HALVES, r=PACK))
 
@@ -147,7 +174,7 @@ def tile_mix_feat_fm_crelupl_gelu_kernel(
                 out=acc[g][:],
                 lhsT=codes["a", a, tt][:].bitcast(FP8X4),
                 lhsT_scale=scales["a", a, tt][:],
-                rhs=w4[a][:, 2 * N_HALF * h : 2 * N_HALF * (h + 1)].bitcast(FP4X4),
+                rhs=w4[a, h].bitcast(FP4X4),
                 rhs_scale=plane[:, N_HALF * h : N_HALF * (h + 1)],
                 start=(a == 0),
                 stop=False,
@@ -179,7 +206,7 @@ def tile_mix_feat_fm_crelupl_gelu_kernel(
                 quantize_x("b", a, tt)
             for g in by_token_tile:
                 product_w4(a, g)
-            for g in by_token_tile:
+            for g in by_token_tile if a < last - 1 else range(T_TILES):
                 product_w8(a, g)
 
         for tt in range(T_TILES):
@@ -195,26 +222,33 @@ def tile_mix_feat_fm_crelupl_gelu_kernel(
         turned = {}
         result = {}
         narrow = {}
-        out_codes = {}
         out_scales = sb.tile([P, M], U8, name="out_scales", align_bytes=64)
+        out_codes = []
+        for h in range(HALVES):
+            out_codes.append(sb.tile([P, T], U32, name="out_codes%d" % h, align_bytes=64))
 
         def finish(g):
+            if g >= T_TILES:
+                product_w8(last - 1, g)
             product_w4(last, g)
             product_w8(last, g)
 
-        def deal(g, on_vector):
+        def deal(g, on_vector, pieces=1):
             dealt[g] = sb.tile([P, PACK, P], F32, name="dealt%d" % g)
             src = acc[g][:].rearrange("t (p r) -> t r p", r=PACK)
-            if on_vector:
-                nc.vector.tensor_copy(out=dealt[g][:], in_=src)
-            else:
-                nc.scalar.copy(out=dealt[g][:], in_=src)
+            step = PACK // pieces
+            for r in range(0, PACK, step):
+                if on_vector:
+                    nc.vector.tensor_copy(out=dealt[g][:, r : r + step, :], in_=src[:, r : r + step, :])
+                else:
+                    nc.scalar.copy(out=dealt[g][:, r : r + step, :], in_=src[:, r : r + step, :])
 
-        def turn(unit):
-            per_bank = PACK // len(unit)
+        def turn(unit, banks):
+            per_bank = PACK // len(banks)
             width = T_TILE * len(unit)
-            for i, g in enumerate(unit):
-                bank = psum.tile([P, per_bank, width], F32, name="turned%d" % g, tag="bank%d" % g)
+            for i, bank_no in enumerate(banks):
+                name = "turned%d_%d" % (unit[0], i)
+                bank = psum.tile([P, per_bank, width], F32, name=name, tag="bank%d" % bank_no)
                 for rr in range(per_bank):
                     r = i * per_bank + rr
                     turned[unit, r] = bank[:, rr, :]
@@ -227,9 +261,10 @@ def tile_mix_feat_fm_crelupl_gelu_kernel(
             h, tt = groups[unit[0]]
             return h, tt * T_TILE, T_TILE * len(unit)
 
-        def gelu(unit):
+        def gelu(unit, rows_per_store):
             h, t0, width = columns(unit)
             result[unit] = sb.tile([P, PACK, width], F32, name="result%d" % unit[0])
+            rows = out_0[N_HALF * h : N_HALF * (h + 1), t0 : t0 + width].rearrange("(p r) t -> p r t", r=PACK)
             for r in range(PACK):
                 nc.scalar.activation(
                     out=result[unit][:, r, :],
@@ -237,11 +272,9 @@ def tile_mix_feat_fm_crelupl_gelu_kernel(
                     func=ACT.Gelu_apprx_tanh,
                     bias=bias[:, h, r : r + 1],
                 )
-
-        def store_result(unit):
-            h, t0, width = columns(unit)
-            rows = out_0[N_HALF * h : N_HALF * (h + 1), t0 : t0 + width]
-            nc.sync.dma_start(out=rows.rearrange("(p r) t -> p r t", r=PACK), in_=result[unit][:])
+                if (r + 1) % rows_per_store == 0:
+                    done = slice(r + 1 - rows_per_store, r + 1)
+                    nc.sync.dma_start(out=rows[:, done, :], in_=result[unit][:, done, :])
 
         def round_result(unit):
             h, t0, width = columns(unit)
@@ -250,67 +283,53 @@ def tile_mix_feat_fm_crelupl_gelu_kernel(
 
         def quantize_result(unit):
             h, t0, width = columns(unit)
-            pair = (h, t0 // (2 * T_TILE))
-            if pair not in out_codes:
-                out_codes[pair] = sb.tile([P, 2 * T_TILE], U32, name="out_codes%d_%d" % pair, align_bytes=64)
-            c0 = t0 - pair[1] * 2 * T_TILE
             nc.vector.quantize_mx(
-                out=out_codes[pair][:, c0 : c0 + width].bitcast(FP8X4),
+                out=out_codes[h][:, t0 : t0 + width].bitcast(FP8X4),
                 scales=out_scales[:, T * h + t0 : T * h + t0 + width],
                 in_=narrow[unit][:],
             )
 
         code_rows = out_1.rearrange("a p t i -> a p (t i)").bitcast(I32)
 
-        def store_codes(pair):
-            h, half = pair
-            t0 = half * 2 * T_TILE
-            nc.sync.dma_start(out=code_rows[h, :, t0 : t0 + 2 * T_TILE], in_=out_codes[pair][:].bitcast(I32))
+        def store_codes(h, t0, t1):
+            nc.sync.dma_start(out=code_rows[h, :, t0:t1], in_=out_codes[h][:, t0:t1].bitcast(I32))
 
-        u01, u23, u45, u6, u7 = (0, 1), (2, 3), (4, 5), (6,), (7,)
-        for g in range(4):
+        first_half = (0, 1, 2, 3)
+        u4, u5, u6, u7 = (4,), (5,), (6,), (7,)
+        for g in first_half:
             finish(g)
-        deal(0, True)
-        deal(1, False)
-        deal(2, True)
-        deal(3, False)
-        turn(u01)
-        turn(u23)
-        gelu(u01)
-        store_result(u01)
+            deal(g, g % 2 == 0)
         finish(4)
+        deal(4, True)
+        turn(first_half, [0, 1, 2, 3])
+        turn(u4, [4])
+        gelu(first_half, 1)
+        gelu(u4, PACK)
         finish(5)
         finish(6)
-        deal(4, True)
-        deal(5, True)
-        gelu(u23)
-        store_result(u23)
-        deal(6, False)
-        turn(u45)
+        round_result(first_half)
+        deal(5, False)
+        deal(6, True)
+        turn(u5, [5])
+        turn(u6, [6])
+        quantize_result(first_half)
+        store_codes(0, 0, T)
+        gelu(u5, PACK)
+        gelu(u6, PACK)
         finish(7)
-        round_result(u01)
-        round_result(u23)
-        quantize_result(u01)
-        store_codes((0, 0))
-        deal(7, True)
-        turn(u6)
-        turn(u7)
-        gelu(u45)
-        store_result(u45)
-        quantize_result(u23)
-        store_codes((0, 1))
-        gelu(u6)
-        store_result(u6)
-        gelu(u7)
-        store_result(u7)
-        round_result(u45)
+        round_result(u4)
+        round_result(u5)
         round_result(u6)
-        quantize_result(u45)
-        store_codes((1, 0))
-        round_result(u7)
+        deal(7, True, PACK)
+        turn(u7, [0, 1, 2, 3])
+        quantize_result(u4)
+        quantize_result(u5)
         quantize_result(u6)
+        store_codes(1, 0, 3 * T_TILE)
+        gelu(u7, PACK)
+        round_result(u7)
         quantize_result(u7)
-        store_codes((1, 1))
+        store_codes(1, 3 * T_TILE, T)
         scale_rows = out_2.bitcast(I32).rearrange("a (g r) t -> r g a t", r=QUADS)
         planes = out_scales[:].bitcast(I32).rearrange("p (a t) -> p a t", a=HALVES)
         for r in range(QUADS):

@@ -40,8 +40,8 @@ def tile_mix_feat_fm_crelupl_gelu_kernel(
         psum = ctx.enter_context(tc.psum_pool(name="psum", bufs=1))
         ctx.enter_context(tc.manual_schedule())
 
-        s4_first = sb.tile([P, M], U8, name="s4_first", align_bytes=64)
-        s4_rest = sb.tile([P, last, M], U8, name="s4_rest", align_bytes=64)
+        s4_first = sb.tile([P, 2, M], U8, name="s4_first", align_bytes=64)
+        s4_rest = sb.tile([P, 2, M], U8, name="s4_rest", align_bytes=64)
         s8 = sb.tile([P, M], U8, name="s8", align_bytes=64)
         ones = sb.tile([P, PACK * P], BF16, name="ones", align_bytes=64)
         warm_codes = sb.tile([P, P], U32, name="warm_codes", align_bytes=64)
@@ -98,26 +98,27 @@ def tile_mix_feat_fm_crelupl_gelu_kernel(
                 for h in halves:
                     w8[a, h] = words[:, i, N_HALF * h - n0 : N_HALF * (h + 1) - n0]
 
-        for r in range(QUADS):
-            nc.scalar.dma_start(out=s4_first[:].bitcast(I32)[r:P:32, :], in_=s4_rows[r, :, 0, :])
-        load_x(0)
-        load_w4([0], [0, 1])
         preload = sb.tile([P, 1], F32, name="preload")
         nc.scalar.activation(out=preload[:], in_=ones[:, 0:1], func=ACT.Gelu_apprx_tanh)
+
+        load_x(0)
+        for r in range(QUADS):
+            nc.sync.dma_start(out=s4_first[:].bitcast(I32)[r:P:32, :, :], in_=s4_rows[r, :, 0:2, :])
+        load_w4([0], [0, 1])
+        load_w8([0], [0, 1])
         for g in range(QUADS):
-            nc.scalar.dma_start(
+            nc.sync.dma_start(
                 out=s8[:].bitcast(I32)[32 * g : 32 * g + 16, :], in_=s8_rows[:, 4 * g : 4 * g + 4, :]
             )
-        load_w8([0], [0, 1])
         load_x(1)
-        for r in range(QUADS):
-            nc.sync.dma_start(out=s4_rest[:].bitcast(I32)[r:P:32, :, :], in_=s4_rows[r, :, 1:PASSES, :])
         load_w4([1], [0, 1])
         load_w8([1], [0, 1])
         load_x(2)
+        for r in range(QUADS):
+            nc.sync.dma_start(out=s4_rest[:].bitcast(I32)[r:P:32, :, :], in_=s4_rows[r, :, 2:PASSES, :])
         load_w4([2], [0, 1])
-        load_w8([2], [0])
         load_x(3)
+        load_w8([2], [0])
         load_w4([3], [0])
         load_w8([3], [0])
         load_w8([2, 3], [1])
@@ -169,7 +170,7 @@ def tile_mix_feat_fm_crelupl_gelu_kernel(
 
         def product_w4(a, g):
             h, tt = groups[g]
-            plane = s4_first[:, :] if a == 0 else s4_rest[:, a - 1, :]
+            plane = s4_first[:, a, :] if a < 2 else s4_rest[:, a - 2, :]
             nc.tensor.matmul_mx(
                 out=acc[g][:],
                 lhsT=codes["a", a, tt][:].bitcast(FP8X4),
@@ -294,42 +295,45 @@ def tile_mix_feat_fm_crelupl_gelu_kernel(
         def store_codes(h, t0, t1):
             nc.sync.dma_start(out=code_rows[h, :, t0:t1], in_=out_codes[h][:, t0:t1].bitcast(I32))
 
-        first_half = (0, 1, 2, 3)
-        u4, u5, u6, u7 = (4,), (5,), (6,), (7,)
-        for g in first_half:
-            finish(g)
-            deal(g, g % 2 == 0)
+        finish(0)
+        deal(0, True)
+        finish(1)
+        deal(1, False)
+        finish(2)
+        deal(2, True)
+        finish(3)
+        deal(3, False)
+        turn((0, 1,), [0, 1])
         finish(4)
+        turn((2, 3,), [2, 3])
+        gelu((0, 1,), 2)
+        gelu((2, 3,), 2)
         deal(4, True)
-        turn(first_half, [0, 1, 2, 3])
-        turn(u4, [4])
-        gelu(first_half, 1)
-        gelu(u4, PACK)
+        round_result((0, 1,))
         finish(5)
-        finish(6)
-        round_result(first_half)
         deal(5, False)
-        deal(6, True)
-        turn(u5, [5])
-        turn(u6, [6])
-        quantize_result(first_half)
-        store_codes(0, 0, T)
-        gelu(u5, PACK)
-        gelu(u6, PACK)
+        finish(6)
+        deal(6, False)
+        quantize_result((0, 1,))
+        round_result((2, 3,))
+        quantize_result((2, 3,))
+        store_codes(0, 0 * T_TILE, 4 * T_TILE)
+        turn((4, 5,), [4, 5])
         finish(7)
-        round_result(u4)
-        round_result(u5)
-        round_result(u6)
+        gelu((4, 5,), 2)
         deal(7, True, PACK)
-        turn(u7, [0, 1, 2, 3])
-        quantize_result(u4)
-        quantize_result(u5)
-        quantize_result(u6)
-        store_codes(1, 0, 3 * T_TILE)
-        gelu(u7, PACK)
-        round_result(u7)
-        quantize_result(u7)
-        store_codes(1, 3 * T_TILE, T)
+        turn((6,), [6])
+        turn((7,), [0, 1, 2, 3])
+        gelu((6,), 4)
+        round_result((4, 5,))
+        gelu((7,), 4)
+        round_result((6,))
+        quantize_result((4, 5,))
+        quantize_result((6,))
+        store_codes(1, 0 * T_TILE, 3 * T_TILE)
+        round_result((7,))
+        quantize_result((7,))
+        store_codes(1, 3 * T_TILE, 4 * T_TILE)
         scale_rows = out_2.bitcast(I32).rearrange("a (g r) t -> r g a t", r=QUADS)
         planes = out_scales[:].bitcast(I32).rearrange("p (a t) -> p a t", a=HALVES)
         for r in range(QUADS):

@@ -136,15 +136,13 @@ def tile_mix_feat_fm_crelupl_gelu_kernel(
         def by_pairs(rows_ap):
             return rows_ap.rearrange("p j (c i) -> p c j i", i=PAIR)
 
-        def positive_part(a, tt):
+        def positive_part(a, tt, on_vector=True):
             dst = sb.tile([P, PACK * T_TILE], BF16, name="xa%d_%d" % (a, tt), align_bytes=64)
-            nc.vector.tensor_scalar(
-                out=grouped(dst[:]),
-                in0=by_pairs(raw[a][:, :, tt * T_TILE : (tt + 1) * T_TILE]),
-                scalar1=0.0,
-                scalar2=None,
-                op0=ALU.max,
-            )
+            src = by_pairs(raw[a][:, :, tt * T_TILE : (tt + 1) * T_TILE])
+            if on_vector:
+                nc.vector.tensor_scalar(out=grouped(dst[:]), in0=src, scalar1=0.0, scalar2=None, op0=ALU.max)
+            else:
+                nc.scalar.activation(out=grouped(dst[:]), in_=src, func=ACT.Relu)
             rounded["a", a, tt] = dst
 
         def negative_part(a, tt):
@@ -158,57 +156,127 @@ def tile_mix_feat_fm_crelupl_gelu_kernel(
             rounded["b", a, tt] = dst
 
         def quantize_x(part, a, tt):
-            key = (part, a, tt)
-            codes[key] = sb.tile([P, T_TILE], U32, name="c%s%d_%d" % key, align_bytes=64)
-            scales[key] = sb.tile([P, T_TILE], U8, name="s%s%d_%d" % key, align_bytes=64)
-            nc.vector.quantize_mx(out=codes[key][:].bitcast(FP8X4), scales=scales[key][:], in_=rounded[key][:])
+            if (part, a) not in codes:
+                codes[part, a] = sb.tile([P, T], U32, name="c%s%d" % (part, a), align_bytes=64)
+                scales[part, a] = sb.tile([P, T], U8, name="s%s%d" % (part, a), align_bytes=64)
+            cols = slice(tt * T_TILE, (tt + 1) * T_TILE)
+            nc.vector.quantize_mx(
+                out=codes[part, a][:, cols].bitcast(FP8X4),
+                scales=scales[part, a][:, cols],
+                in_=rounded[part, a, tt][:],
+            )
 
         groups = [(h, tt) for h in range(HALVES) for tt in range(T_TILES)]
         acc = []
         for g in range(len(groups)):
             acc.append(psum.tile([P, N_HALF], F32, name="acc%d" % g, tag="bank%d" % g))
 
-        def product_w4(a, g):
-            h, tt = groups[g]
+        def product_w4(a, tt):
+            cols = slice(tt * T_TILE, (tt + 1) * T_TILE)
             plane = s4_first[:, a, :] if a < 2 else s4_rest[:, a - 2, :]
             nc.tensor.matmul_mx(
-                out=acc[g][:],
-                lhsT=codes["a", a, tt][:].bitcast(FP8X4),
-                lhsT_scale=scales["a", a, tt][:],
-                rhs=w4[a, h].bitcast(FP4X4),
-                rhs_scale=plane[:, N_HALF * h : N_HALF * (h + 1)],
+                out=acc[tt][:],
+                lhsT=codes["a", a][:, cols].bitcast(FP8X4),
+                lhsT_scale=scales["a", a][:, cols],
+                rhs=w4[a, 0].bitcast(FP4X4),
+                rhs_scale=plane[:, 0:N_HALF],
                 start=(a == 0),
                 stop=False,
             )
 
-        def product_w8(a, g):
-            h, tt = groups[g]
+        def product_w8(a, tt):
+            cols = slice(tt * T_TILE, (tt + 1) * T_TILE)
             nc.tensor.matmul_mx(
-                out=acc[g][:],
-                lhsT=codes["b", a, tt][:].bitcast(FP8X4),
-                lhsT_scale=scales["b", a, tt][:],
-                rhs=w8[a, h].bitcast(FP8X4),
-                rhs_scale=s8[4 * a : P, N_HALF * h : N_HALF * (h + 1)],
+                out=acc[tt][:],
+                lhsT=codes["b", a][:, cols].bitcast(FP8X4),
+                lhsT_scale=scales["b", a][:, cols],
+                rhs=w8[a, 0].bitcast(FP8X4),
+                rhs_scale=s8[4 * a : P, 0:N_HALF],
                 start=False,
                 stop=(a == last),
             )
 
-        by_token_tile = [h * T_TILES + tt for tt in range(T_TILES) for h in range(HALVES)]
+        w4d = {}
+        w8d = {}
+        s4d = {}
+        s8d = sb.tile([P, PACK, P], U8, name="s8d", align_bytes=64)
+
+        def deal_w4(a):
+            w4d[a] = sb.tile([P, PACK, 2 * P], U8, name="w4d%d" % a, align_bytes=64)
+            nc.vector.tensor_copy(
+                out=w4d[a][:].rearrange("p r (m b) -> p r m b", b=2),
+                in_=w4[a, 1].rearrange("p (m r b) -> p r m b", r=PACK, b=2),
+            )
+
+        def deal_w8(a):
+            w8d[a] = sb.tile([P, PACK, P], U32, name="w8d%d" % a, align_bytes=64)
+            nc.vector.tensor_copy(
+                out=w8d[a][:].bitcast(I32).rearrange("p r (c i) -> p c r i", i=4),
+                in_=w8[a, 1].bitcast(I32).rearrange("p (c i r) -> p c r i", i=4, r=PACK),
+            )
+
+        def deal_s4(a0, planes):
+            both = sb.tile([P, 2, PACK, P], U8, name="s4d%d" % a0, align_bytes=64)
+            nc.vector.tensor_copy(
+                out=both[:], in_=planes[:, :, N_HALF:M].rearrange("p a (m r) -> p a r m", r=PACK)
+            )
+            s4d[a0] = both[:, 0, :, :]
+            s4d[a0 + 1] = both[:, 1, :, :]
+
+        def deal_s8():
+            nc.vector.tensor_copy(out=s8d[:], in_=s8[:, N_HALF:M].rearrange("p (m r) -> p r m", r=PACK))
+
+        def dealt_w4(a, r):
+            nc.tensor.matmul_mx(
+                out=acc[T_TILES + r][:],
+                lhsT=w4d[a][:, r, :].bitcast(FP4X4),
+                lhsT_scale=s4d[a][:, r, :],
+                rhs=codes["a", a][:].bitcast(FP8X4),
+                rhs_scale=scales["a", a][:],
+                start=(a == 0),
+                stop=(a == last),
+            )
+
+        def dealt_w8(a, r):
+            nc.tensor.matmul_mx(
+                out=acc[T_TILES + r][:],
+                lhsT=w8d[a][:, r, :].bitcast(FP8X4),
+                lhsT_scale=s8d[4 * a : P, r, :],
+                rhs=codes["b", a][:].bitcast(FP8X4),
+                rhs_scale=scales["b", a][:],
+                start=False,
+                stop=False,
+            )
+
         for a in range(last):
+            positive_part(a, T_TILES - 1, False)
             for tt in range(T_TILES):
                 negative_part(a, tt)
             positive_part(a, 0)
+            positive_part(a, 1)
+            quantize_x("a", a, 0)
+            positive_part(a, 2)
             for tt in range(1, T_TILES):
-                positive_part(a, tt)
-                quantize_x("a", a, tt - 1)
-            quantize_x("b", a, 0)
-            quantize_x("a", a, T_TILES - 1)
-            for tt in range(1, T_TILES):
+                quantize_x("a", a, tt)
+            if a % 2 == 0:
+                deal_s4(a, s4_first if a == 0 else s4_rest)
+            deal_w4(a)
+            for tt in range(T_TILES):
                 quantize_x("b", a, tt)
-            for g in by_token_tile:
-                product_w4(a, g)
-            for g in by_token_tile if a < last - 1 else range(T_TILES):
-                product_w8(a, g)
+            if a == 0:
+                deal_s8()
+            for tt in range(T_TILES):
+                product_w4(a, tt)
+            for r in range(PACK):
+                dealt_w4(a, r)
+            if a < last - 1:
+                deal_w8(a)
+                for tt in range(T_TILES):
+                    product_w8(a, tt)
+                for r in range(PACK):
+                    dealt_w8(a, r)
+        for tt in range(T_TILES):
+            product_w8(last - 1, tt)
 
         for tt in range(T_TILES):
             negative_part(last, tt)
@@ -229,10 +297,44 @@ def tile_mix_feat_fm_crelupl_gelu_kernel(
             out_codes.append(sb.tile([P, T], U32, name="out_codes%d" % h, align_bytes=64))
 
         def finish(g):
-            if g >= T_TILES:
-                product_w8(last - 1, g)
             product_w4(last, g)
             product_w8(last, g)
+
+        def finish_dealt(r):
+            dealt_w8(last - 1, r)
+            dealt_w8(last, r)
+            dealt_w4(last, r)
+
+        high = sb.tile([P, PACK, T], F32, name="high")
+        high_rows = out_0[N_HALF:M, :].rearrange("(p r) t -> p r t", r=PACK)
+        high_narrow = {}
+
+        def gelu_dealt(r, pieces):
+            step = T // pieces
+            for t0 in range(0, T, step):
+                nc.scalar.activation(
+                    out=high[:, r, t0 : t0 + step],
+                    in_=acc[T_TILES + r][:, t0 : t0 + step],
+                    func=ACT.Gelu_apprx_tanh,
+                    bias=bias[:, 1, r : r + 1],
+                )
+            nc.sync.dma_start(out=high_rows[:, r, :], in_=high[:, r, :])
+
+        def round_high(t0, t1, on_vector):
+            cols = slice(t0 * T_TILE, t1 * T_TILE)
+            dst = sb.tile([P, PACK * (t1 - t0) * T_TILE], BF16, name="high_narrow%d" % t0, align_bytes=64)
+            high_narrow[t0] = dst
+            if on_vector:
+                nc.vector.tensor_copy(out=grouped(dst[:]), in_=by_pairs(high[:, :, cols]))
+            else:
+                nc.scalar.copy(out=grouped(dst[:]), in_=by_pairs(high[:, :, cols]))
+
+        def quantize_high(t0, t1):
+            nc.vector.quantize_mx(
+                out=out_codes[1][:, t0 * T_TILE : t1 * T_TILE].bitcast(FP8X4),
+                scales=out_scales[:, T + t0 * T_TILE : T + t1 * T_TILE],
+                in_=high_narrow[t0][:],
+            )
 
         def deal(g, on_vector, pieces=1):
             dealt[g] = sb.tile([P, PACK, P], F32, name="dealt%d" % g)
@@ -300,40 +402,37 @@ def tile_mix_feat_fm_crelupl_gelu_kernel(
         finish(1)
         deal(1, False)
         finish(2)
-        deal(2, True)
+        deal_w8(2)
+        deal_w8(3)
+        deal(2, False)
         finish(3)
-        deal(3, False)
+        deal_w4(3)
+        deal(3, True)
         turn((0, 1,), [0, 1])
-        finish(4)
-        turn((2, 3,), [2, 3])
         gelu((0, 1,), 2)
+        finish_dealt(0)
+        turn((2, 3,), [2, 3])
+        gelu_dealt(0, 1)
         gelu((2, 3,), 2)
-        deal(4, True)
+        finish_dealt(1)
+        finish_dealt(2)
+        finish_dealt(3)
         round_result((0, 1,))
-        finish(5)
-        deal(5, False)
-        finish(6)
-        deal(6, False)
+        gelu_dealt(1, 1)
         quantize_result((0, 1,))
         round_result((2, 3,))
+        gelu_dealt(2, 1)
         quantize_result((2, 3,))
         store_codes(0, 0 * T_TILE, 4 * T_TILE)
-        turn((4, 5,), [4, 5])
-        finish(7)
-        gelu((4, 5,), 2)
-        deal(7, True, PACK)
-        turn((6,), [6])
-        turn((7,), [0, 1, 2, 3])
-        gelu((6,), 4)
-        round_result((4, 5,))
-        gelu((7,), 4)
-        round_result((6,))
-        quantize_result((4, 5,))
-        quantize_result((6,))
-        store_codes(1, 0 * T_TILE, 3 * T_TILE)
-        round_result((7,))
-        quantize_result((7,))
-        store_codes(1, 3 * T_TILE, 4 * T_TILE)
+        gelu_dealt(3, 2)
+        round_high(0, 2, True)
+        round_high(3, 4, False)
+        round_high(2, 3, True)
+        quantize_high(0, 2)
+        store_codes(1, 0 * T_TILE, 2 * T_TILE)
+        quantize_high(2, 3)
+        quantize_high(3, 4)
+        store_codes(1, 2 * T_TILE, 4 * T_TILE)
         scale_rows = out_2.bitcast(I32).rearrange("a (g r) t -> r g a t", r=QUADS)
         planes = out_scales[:].bitcast(I32).rearrange("p (a t) -> p a t", a=HALVES)
         for r in range(QUADS):

@@ -20,53 +20,43 @@ P = 128
 PACK = 4
 K_PASS = P * PACK
 PASSES = K // K_PASS
+LAST = PASSES - 1
 T_TILE = 128
 T_TILES = T // T_TILE
 N_HALF = 512
-HALVES = M // N_HALF
-QUADS = 4
-PAIR = 2
-WARM_UP_PASSES = 32
+LOW, HIGH = 0, 1
+QUADRANT = 32
+SCALE_ROWS = 4
+PASS_PAIR = 2
+RUN = 2
+LINE_WORDS = 4
 
 
 def tile_mix_feat_fm_crelupl_gelu_kernel(
     tc, x, w4_words, w4_scales, w8_words, w8_scales, b, out_0, out_1, out_2
 ):
     nc = tc.nc
-    last = PASSES - 1
 
     with ExitStack() as ctx:
         sb = ctx.enter_context(tc.tile_pool(name="sb", bufs=1))
         psum = ctx.enter_context(tc.psum_pool(name="psum", bufs=1))
         ctx.enter_context(tc.manual_schedule())
 
-        s4_first = sb.tile([P, 2, M], U8, name="s4_first", align_bytes=64)
-        s4_rest = sb.tile([P, 2, M], U8, name="s4_rest", align_bytes=64)
-        s8 = sb.tile([P, M], U8, name="s8", align_bytes=64)
-        ones = sb.tile([P, PACK * P], BF16, name="ones", align_bytes=64)
-        warm_codes = sb.tile([P, P], U32, name="warm_codes", align_bytes=64)
-        warm_scales = sb.tile([P, P], U8, name="warm_scales", align_bytes=64)
-        nc.vector.memset(ones[:], 1.0)
-        nc.vector.memset(s4_first[:].bitcast(I32), 0)
-        nc.vector.quantize_mx(out=warm_codes[:].bitcast(FP8X4), scales=warm_scales[:], in_=ones[:])
-        nc.vector.memset(s8[:].bitcast(I32), 0)
-        nc.vector.memset(s4_rest[:].bitcast(I32), 0)
+        w4_planes = []
+        for i in range(PASSES // PASS_PAIR):
+            w4_planes.append(sb.tile([P, PASS_PAIR, M], U8, name="w4_planes%d" % i, align_bytes=64))
+        w8_planes = sb.tile([P, M], U8, name="w8_planes", align_bytes=64)
+        nc.vector.memset(w4_planes[0][:].bitcast(I32), 0)
+        nc.vector.memset(w8_planes[:].bitcast(I32), 0)
+        nc.vector.memset(w4_planes[1][:].bitcast(I32), 0)
         ident = sb.tile([P, P], F32, name="ident")
         make_identity(nc, ident[:])
-        warm = psum.tile([P, P], F32, name="warm", tag="bank7")
-        for i in range(WARM_UP_PASSES):
-            nc.tensor.matmul_mx(
-                out=warm[:],
-                lhsT=warm_codes[:].bitcast(FP8X4),
-                lhsT_scale=warm_scales[:],
-                rhs=warm_codes[:].bitcast(FP8X4),
-                rhs_scale=warm_scales[:],
-                start=True,
-                stop=True,
-            )
 
-        s4_rows = w4_scales.bitcast(I32).rearrange("a (g r) n -> r g a n", r=QUADS)
-        s8_rows = w8_scales.bitcast(I32)
+        preload = sb.tile([P, 1], F32, name="preload")
+        nc.scalar.activation(out=preload[:], in_=ident[:, 0:1], func=ACT.Gelu_apprx_tanh)
+
+        w4_scale_rows = w4_scales.bitcast(I32).rearrange("a (g s) n -> s g a n", s=SCALE_ROWS)
+        w8_scale_rows = w8_scales.bitcast(I32)
         w4_rows = w4_words.bitcast(I32).rearrange("a p n -> p a n")
         w8_rows = w8_words.rearrange("a p n i -> p a (n i)").bitcast(I32)
         raw = {}
@@ -78,363 +68,339 @@ def tile_mix_feat_fm_crelupl_gelu_kernel(
             rows = x[a * K_PASS : (a + 1) * K_PASS, :]
             nc.sync.dma_start(out=raw[a][:], in_=rows.rearrange("(p j) t -> p j t", j=PACK))
 
-        def load_w4(passes, halves):
+        def load_w4(a, halves):
             n0, n1 = N_HALF * halves[0], N_HALF * (halves[-1] + 1)
-            name = "w4_%d_%d" % (passes[0], halves[0])
-            words = sb.tile([P, len(passes), 2 * (n1 - n0)], U8, name=name, align_bytes=64)
-            src = w4_rows[:, passes[0] : passes[-1] + 1, n0 // 2 : n1 // 2]
-            nc.sync.dma_start(out=words[:].bitcast(I32), in_=src)
-            for i, a in enumerate(passes):
-                for h in halves:
-                    w4[a, h] = words[:, i, 2 * (N_HALF * h - n0) : 2 * (N_HALF * (h + 1) - n0)]
+            words = sb.tile([P, 1, 2 * (n1 - n0)], U8, name="w4_%d_%d" % (a, halves[0]), align_bytes=64)
+            nc.sync.dma_start(out=words[:].bitcast(I32), in_=w4_rows[:, a : a + 1, n0 // 2 : n1 // 2])
+            for h in halves:
+                w4[a, h] = words[:, 0, 2 * (N_HALF * h - n0) : 2 * (N_HALF * (h + 1) - n0)]
 
         def load_w8(passes, halves):
             n0, n1 = N_HALF * halves[0], N_HALF * (halves[-1] + 1)
             name = "w8_%d_%d" % (passes[0], halves[0])
             words = sb.tile([P, len(passes), n1 - n0], U32, name=name, align_bytes=64)
-            src = w8_rows[:, passes[0] : passes[-1] + 1, n0:n1]
-            nc.sync.dma_start(out=words[:].bitcast(I32), in_=src)
+            nc.sync.dma_start(out=words[:].bitcast(I32), in_=w8_rows[:, passes[0] : passes[-1] + 1, n0:n1])
             for i, a in enumerate(passes):
                 for h in halves:
                     w8[a, h] = words[:, i, N_HALF * h - n0 : N_HALF * (h + 1) - n0]
 
-        preload = sb.tile([P, 1], F32, name="preload")
-        nc.scalar.activation(out=preload[:], in_=ones[:, 0:1], func=ACT.Gelu_apprx_tanh)
+        def load_w4_planes(i):
+            for s in range(SCALE_ROWS):
+                nc.sync.dma_start(
+                    out=w4_planes[i][:].bitcast(I32)[s:P:QUADRANT, :, :],
+                    in_=w4_scale_rows[s, :, PASS_PAIR * i : PASS_PAIR * (i + 1), :],
+                )
+
+        def load_w8_planes():
+            for g in range(P // QUADRANT):
+                nc.sync.dma_start(
+                    out=w8_planes[:].bitcast(I32)[QUADRANT * g : QUADRANT * g + SCALE_ROWS * PASSES, :],
+                    in_=w8_scale_rows[:, SCALE_ROWS * g : SCALE_ROWS * (g + 1), :],
+                )
 
         load_x(0)
-        for r in range(QUADS):
-            nc.sync.dma_start(out=s4_first[:].bitcast(I32)[r:P:32, :, :], in_=s4_rows[r, :, 0:2, :])
-        load_w4([0], [0, 1])
-        load_w8([0], [0, 1])
-        for g in range(QUADS):
-            nc.sync.dma_start(
-                out=s8[:].bitcast(I32)[32 * g : 32 * g + 16, :], in_=s8_rows[:, 4 * g : 4 * g + 4, :]
-            )
+        load_w4_planes(0)
+        load_w4(0, [LOW, HIGH])
+        load_w8([0], [LOW, HIGH])
+        load_w8_planes()
         load_x(1)
-        load_w4([1], [0, 1])
-        load_w8([1], [0, 1])
+        load_w4(1, [LOW, HIGH])
+        load_w8([1], [LOW, HIGH])
         load_x(2)
-        for r in range(QUADS):
-            nc.sync.dma_start(out=s4_rest[:].bitcast(I32)[r:P:32, :, :], in_=s4_rows[r, :, 2:PASSES, :])
-        load_w4([2], [0, 1])
-        load_x(3)
-        load_w8([2], [0])
-        load_w4([3], [0])
-        load_w8([3], [0])
-        load_w8([2, 3], [1])
-        load_w4([3], [1])
-        bias = sb.tile([P, HALVES, PACK], F32, name="bias")
-        nc.sync.dma_start(out=bias[:], in_=b.rearrange("(h p r) -> p h r", h=HALVES, r=PACK))
+        load_w4_planes(1)
+        load_w4(2, [LOW, HIGH])
+        load_x(LAST)
+        load_w8([LAST - 1], [LOW])
+        load_w4(LAST, [LOW])
+        load_w8([LAST], [LOW])
+        load_w8([LAST - 1, LAST], [HIGH])
+        load_w4(LAST, [HIGH])
+        bias = sb.tile([P, M // N_HALF, PACK], F32, name="bias")
+        nc.sync.dma_start(out=bias[:], in_=b.rearrange("(h p r) -> p h r", h=M // N_HALF, r=PACK))
+
+        def as_words(narrow_ap):
+            return narrow_ap.rearrange("p (c i j) -> p c j i", i=RUN, j=PACK)
+
+        def as_rows(wide_ap):
+            return wide_ap.rearrange("p j (c i) -> p c j i", i=RUN)
+
+        def t_cols(tt0, tt1):
+            return slice(tt0 * T_TILE, tt1 * T_TILE)
 
         rounded = {}
         codes = {}
-        scales = {}
+        planes = {}
 
-        def grouped(tile_ap):
-            return tile_ap.rearrange("p (c i j) -> p c j i", i=PAIR, j=PACK)
-
-        def by_pairs(rows_ap):
-            return rows_ap.rearrange("p j (c i) -> p c j i", i=PAIR)
-
-        def positive_part(a, tt, on_vector=True):
+        def positive_part(a, tt, on_vector):
             dst = sb.tile([P, PACK * T_TILE], BF16, name="xa%d_%d" % (a, tt), align_bytes=64)
-            src = by_pairs(raw[a][:, :, tt * T_TILE : (tt + 1) * T_TILE])
+            src = as_rows(raw[a][:, :, t_cols(tt, tt + 1)])
             if on_vector:
-                nc.vector.tensor_scalar(out=grouped(dst[:]), in0=src, scalar1=0.0, scalar2=None, op0=ALU.max)
+                nc.vector.tensor_scalar(out=as_words(dst[:]), in0=src, scalar1=0.0, scalar2=None, op0=ALU.max)
             else:
-                nc.scalar.activation(out=grouped(dst[:]), in_=src, func=ACT.Relu)
+                nc.scalar.activation(out=as_words(dst[:]), in_=src, func=ACT.Relu)
             rounded["a", a, tt] = dst
 
         def negative_part(a, tt):
             dst = sb.tile([P, PACK * T_TILE], BF16, name="xb%d_%d" % (a, tt), align_bytes=64)
-            nc.scalar.activation(
-                out=grouped(dst[:]),
-                in_=by_pairs(raw[a][:, :, tt * T_TILE : (tt + 1) * T_TILE]),
-                func=ACT.Relu,
-                scale=-1.0,
-            )
+            src = as_rows(raw[a][:, :, t_cols(tt, tt + 1)])
+            nc.scalar.activation(out=as_words(dst[:]), in_=src, func=ACT.Relu, scale=-1.0)
             rounded["b", a, tt] = dst
 
         def quantize_x(part, a, tt):
             if (part, a) not in codes:
-                codes[part, a] = sb.tile([P, T], U32, name="c%s%d" % (part, a), align_bytes=64)
-                scales[part, a] = sb.tile([P, T], U8, name="s%s%d" % (part, a), align_bytes=64)
-            cols = slice(tt * T_TILE, (tt + 1) * T_TILE)
+                codes[part, a] = sb.tile([P, T], U32, name="codes_%s%d" % (part, a), align_bytes=64)
+                planes[part, a] = sb.tile([P, T], U8, name="plane_%s%d" % (part, a), align_bytes=64)
             nc.vector.quantize_mx(
-                out=codes[part, a][:, cols].bitcast(FP8X4),
-                scales=scales[part, a][:, cols],
+                out=codes[part, a][:, t_cols(tt, tt + 1)].bitcast(FP8X4),
+                scales=planes[part, a][:, t_cols(tt, tt + 1)],
                 in_=rounded[part, a, tt][:],
             )
 
-        groups = [(h, tt) for h in range(HALVES) for tt in range(T_TILES)]
-        acc = []
-        for g in range(len(groups)):
-            acc.append(psum.tile([P, N_HALF], F32, name="acc%d" % g, tag="bank%d" % g))
+        low_sum = []
+        for tt in range(T_TILES):
+            low_sum.append(psum.tile([P, N_HALF], F32, name="low_sum%d" % tt, tag="bank%d" % tt))
+        high_sum = []
+        for r in range(PACK):
+            high_sum.append(psum.tile([P, T], F32, name="high_sum%d" % r, tag="bank%d" % (T_TILES + r)))
 
-        def product_w4(a, tt):
-            cols = slice(tt * T_TILE, (tt + 1) * T_TILE)
-            plane = s4_first[:, a, :] if a < 2 else s4_rest[:, a - 2, :]
+        def low_w4(a, tt):
             nc.tensor.matmul_mx(
-                out=acc[tt][:],
-                lhsT=codes["a", a][:, cols].bitcast(FP8X4),
-                lhsT_scale=scales["a", a][:, cols],
-                rhs=w4[a, 0].bitcast(FP4X4),
-                rhs_scale=plane[:, 0:N_HALF],
+                out=low_sum[tt][:],
+                lhsT=codes["a", a][:, t_cols(tt, tt + 1)].bitcast(FP8X4),
+                lhsT_scale=planes["a", a][:, t_cols(tt, tt + 1)],
+                rhs=w4[a, LOW].bitcast(FP4X4),
+                rhs_scale=w4_planes[a // PASS_PAIR][:, a % PASS_PAIR, 0:N_HALF],
                 start=(a == 0),
                 stop=False,
             )
 
-        def product_w8(a, tt):
-            cols = slice(tt * T_TILE, (tt + 1) * T_TILE)
+        def low_w8(a, tt):
             nc.tensor.matmul_mx(
-                out=acc[tt][:],
-                lhsT=codes["b", a][:, cols].bitcast(FP8X4),
-                lhsT_scale=scales["b", a][:, cols],
-                rhs=w8[a, 0].bitcast(FP8X4),
-                rhs_scale=s8[4 * a : P, 0:N_HALF],
+                out=low_sum[tt][:],
+                lhsT=codes["b", a][:, t_cols(tt, tt + 1)].bitcast(FP8X4),
+                lhsT_scale=planes["b", a][:, t_cols(tt, tt + 1)],
+                rhs=w8[a, LOW].bitcast(FP8X4),
+                rhs_scale=w8_planes[SCALE_ROWS * a : P, 0:N_HALF],
                 start=False,
-                stop=(a == last),
+                stop=(a == LAST),
             )
 
-        w4d = {}
-        w8d = {}
-        s4d = {}
-        s8d = sb.tile([P, PACK, P], U8, name="s8d", align_bytes=64)
+        w4_dealt = {}
+        w8_dealt = {}
+        w4_plane_dealt = {}
+        w8_planes_dealt = sb.tile([P, PACK, P], U8, name="w8_planes_dealt", align_bytes=64)
 
         def deal_w4(a):
-            w4d[a] = sb.tile([P, PACK, 2 * P], U8, name="w4d%d" % a, align_bytes=64)
+            w4_dealt[a] = sb.tile([P, PACK, 2 * P], U8, name="w4_dealt%d" % a, align_bytes=64)
             nc.vector.tensor_copy(
-                out=w4d[a][:].rearrange("p r (m b) -> p r m b", b=2),
-                in_=w4[a, 1].rearrange("p (m r b) -> p r m b", r=PACK, b=2),
+                out=w4_dealt[a][:].rearrange("p r (m e) -> p r m e", e=2),
+                in_=w4[a, HIGH].rearrange("p (m r e) -> p r m e", r=PACK, e=2),
             )
 
         def deal_w8(a):
-            w8d[a] = sb.tile([P, PACK, P], U32, name="w8d%d" % a, align_bytes=64)
+            w8_dealt[a] = sb.tile([P, PACK, P], U32, name="w8_dealt%d" % a, align_bytes=64)
             nc.vector.tensor_copy(
-                out=w8d[a][:].bitcast(I32).rearrange("p r (c i) -> p c r i", i=4),
-                in_=w8[a, 1].bitcast(I32).rearrange("p (c i r) -> p c r i", i=4, r=PACK),
+                out=w8_dealt[a][:].bitcast(I32).rearrange("p r (c i) -> p c r i", i=LINE_WORDS),
+                in_=w8[a, HIGH].bitcast(I32).rearrange("p (c i r) -> p c r i", i=LINE_WORDS, r=PACK),
             )
 
-        def deal_s4(a0, planes):
-            both = sb.tile([P, 2, PACK, P], U8, name="s4d%d" % a0, align_bytes=64)
+        def deal_w4_planes(i):
+            pair = sb.tile([P, PASS_PAIR, PACK, P], U8, name="w4_planes_dealt%d" % i, align_bytes=64)
             nc.vector.tensor_copy(
-                out=both[:], in_=planes[:, :, N_HALF:M].rearrange("p a (m r) -> p a r m", r=PACK)
+                out=pair[:], in_=w4_planes[i][:, :, N_HALF:M].rearrange("p a (m r) -> p a r m", r=PACK)
             )
-            s4d[a0] = both[:, 0, :, :]
-            s4d[a0 + 1] = both[:, 1, :, :]
+            for j in range(PASS_PAIR):
+                w4_plane_dealt[PASS_PAIR * i + j] = pair[:, j, :, :]
 
-        def deal_s8():
-            nc.vector.tensor_copy(out=s8d[:], in_=s8[:, N_HALF:M].rearrange("p (m r) -> p r m", r=PACK))
+        def deal_w8_planes():
+            nc.vector.tensor_copy(
+                out=w8_planes_dealt[:], in_=w8_planes[:, N_HALF:M].rearrange("p (m r) -> p r m", r=PACK)
+            )
 
-        def dealt_w4(a, r):
+        def high_w4(a, r):
             nc.tensor.matmul_mx(
-                out=acc[T_TILES + r][:],
-                lhsT=w4d[a][:, r, :].bitcast(FP4X4),
-                lhsT_scale=s4d[a][:, r, :],
+                out=high_sum[r][:],
+                lhsT=w4_dealt[a][:, r, :].bitcast(FP4X4),
+                lhsT_scale=w4_plane_dealt[a][:, r, :],
                 rhs=codes["a", a][:].bitcast(FP8X4),
-                rhs_scale=scales["a", a][:],
+                rhs_scale=planes["a", a][:],
                 start=(a == 0),
-                stop=(a == last),
+                stop=(a == LAST),
             )
 
-        def dealt_w8(a, r):
+        def high_w8(a, r):
             nc.tensor.matmul_mx(
-                out=acc[T_TILES + r][:],
-                lhsT=w8d[a][:, r, :].bitcast(FP8X4),
-                lhsT_scale=s8d[4 * a : P, r, :],
+                out=high_sum[r][:],
+                lhsT=w8_dealt[a][:, r, :].bitcast(FP8X4),
+                lhsT_scale=w8_planes_dealt[SCALE_ROWS * a : P, r, :],
                 rhs=codes["b", a][:].bitcast(FP8X4),
-                rhs_scale=scales["b", a][:],
+                rhs_scale=planes["b", a][:],
                 start=False,
                 stop=False,
             )
 
-        for a in range(last):
+        for a in range(LAST):
             positive_part(a, T_TILES - 1, False)
             for tt in range(T_TILES):
                 negative_part(a, tt)
-            positive_part(a, 0)
-            positive_part(a, 1)
+            positive_part(a, 0, True)
+            positive_part(a, 1, True)
             quantize_x("a", a, 0)
-            positive_part(a, 2)
+            positive_part(a, 2, True)
             for tt in range(1, T_TILES):
                 quantize_x("a", a, tt)
-            if a % 2 == 0:
-                deal_s4(a, s4_first if a == 0 else s4_rest)
+            if a % PASS_PAIR == 0:
+                deal_w4_planes(a // PASS_PAIR)
             deal_w4(a)
             for tt in range(T_TILES):
                 quantize_x("b", a, tt)
             if a == 0:
-                deal_s8()
+                deal_w8_planes()
             for tt in range(T_TILES):
-                product_w4(a, tt)
+                low_w4(a, tt)
             for r in range(PACK):
-                dealt_w4(a, r)
-            if a < last - 1:
+                high_w4(a, r)
+            if a < LAST - 1:
                 deal_w8(a)
-                for tt in range(T_TILES):
-                    product_w8(a, tt)
+            for tt in range(T_TILES):
+                low_w8(a, tt)
+            if a < LAST - 1:
                 for r in range(PACK):
-                    dealt_w8(a, r)
-        for tt in range(T_TILES):
-            product_w8(last - 1, tt)
+                    high_w8(a, r)
 
         for tt in range(T_TILES):
-            negative_part(last, tt)
-        positive_part(last, 0)
+            negative_part(LAST, tt)
+        positive_part(LAST, 0, True)
         for tt in range(T_TILES):
             if tt + 1 < T_TILES:
-                positive_part(last, tt + 1)
-            quantize_x("a", last, tt)
-            quantize_x("b", last, tt)
+                positive_part(LAST, tt + 1, True)
+            quantize_x("a", LAST, tt)
+            quantize_x("b", LAST, tt)
 
-        dealt = {}
-        turned = {}
-        result = {}
-        narrow = {}
-        out_scales = sb.tile([P, M], U8, name="out_scales", align_bytes=64)
+        out_plane = sb.tile([P, M // N_HALF * T], U8, name="out_plane", align_bytes=64)
         out_codes = []
-        for h in range(HALVES):
+        for h in (LOW, HIGH):
             out_codes.append(sb.tile([P, T], U32, name="out_codes%d" % h, align_bytes=64))
+        high_out = sb.tile([P, PACK, T], F32, name="high_out")
+        out_rows = out_0.rearrange("(h p r) t -> h p r t", h=M // N_HALF, r=PACK)
+        code_rows = out_1.rearrange("a p t i -> a p (t i)").bitcast(I32)
+        sorted_sum = {}
+        turned = {}
+        low_out = {}
+        narrow = {}
 
-        def finish(g):
-            product_w4(last, g)
-            product_w8(last, g)
+        def finish_low(tt):
+            low_w4(LAST, tt)
+            low_w8(LAST, tt)
 
-        def finish_dealt(r):
-            dealt_w8(last - 1, r)
-            dealt_w8(last, r)
-            dealt_w4(last, r)
+        def finish_high(r):
+            high_w8(LAST - 1, r)
+            high_w8(LAST, r)
+            high_w4(LAST, r)
 
-        high = sb.tile([P, PACK, T], F32, name="high")
-        high_rows = out_0[N_HALF:M, :].rearrange("(p r) t -> p r t", r=PACK)
-        high_narrow = {}
-
-        def gelu_dealt(r, pieces):
-            step = T // pieces
-            for t0 in range(0, T, step):
-                nc.scalar.activation(
-                    out=high[:, r, t0 : t0 + step],
-                    in_=acc[T_TILES + r][:, t0 : t0 + step],
-                    func=ACT.Gelu_apprx_tanh,
-                    bias=bias[:, 1, r : r + 1],
-                )
-            nc.sync.dma_start(out=high_rows[:, r, :], in_=high[:, r, :])
-
-        def round_high(t0, t1, on_vector):
-            cols = slice(t0 * T_TILE, t1 * T_TILE)
-            dst = sb.tile([P, PACK * (t1 - t0) * T_TILE], BF16, name="high_narrow%d" % t0, align_bytes=64)
-            high_narrow[t0] = dst
+        def sort_low(tt, on_vector):
+            sorted_sum[tt] = sb.tile([P, PACK, P], F32, name="sorted_sum%d" % tt)
+            src = low_sum[tt][:].rearrange("t (p r) -> t r p", r=PACK)
             if on_vector:
-                nc.vector.tensor_copy(out=grouped(dst[:]), in_=by_pairs(high[:, :, cols]))
+                nc.vector.tensor_copy(out=sorted_sum[tt][:], in_=src)
             else:
-                nc.scalar.copy(out=grouped(dst[:]), in_=by_pairs(high[:, :, cols]))
+                nc.scalar.copy(out=sorted_sum[tt][:], in_=src)
 
-        def quantize_high(t0, t1):
-            nc.vector.quantize_mx(
-                out=out_codes[1][:, t0 * T_TILE : t1 * T_TILE].bitcast(FP8X4),
-                scales=out_scales[:, T + t0 * T_TILE : T + t1 * T_TILE],
-                in_=high_narrow[t0][:],
-            )
+        def turn_low(tt0):
+            for i in range(2):
+                name = "turned%d" % (tt0 + i)
+                bank = psum.tile([P, 2, 2 * T_TILE], F32, name=name, tag="bank%d" % (tt0 + i))
+                for rr in range(2):
+                    turned[tt0, 2 * i + rr] = bank[:, rr, :]
+                    for j in range(2):
+                        src = sorted_sum[tt0 + j][:, 2 * i + rr, :]
+                        nc.tensor.transpose(bank[:, rr, t_cols(j, j + 1)], src, ident[:])
 
-        def deal(g, on_vector, pieces=1):
-            dealt[g] = sb.tile([P, PACK, P], F32, name="dealt%d" % g)
-            src = acc[g][:].rearrange("t (p r) -> t r p", r=PACK)
-            step = PACK // pieces
-            for r in range(0, PACK, step):
-                if on_vector:
-                    nc.vector.tensor_copy(out=dealt[g][:, r : r + step, :], in_=src[:, r : r + step, :])
-                else:
-                    nc.scalar.copy(out=dealt[g][:, r : r + step, :], in_=src[:, r : r + step, :])
-
-        def turn(unit, banks):
-            per_bank = PACK // len(banks)
-            width = T_TILE * len(unit)
-            for i, bank_no in enumerate(banks):
-                name = "turned%d_%d" % (unit[0], i)
-                bank = psum.tile([P, per_bank, width], F32, name=name, tag="bank%d" % bank_no)
-                for rr in range(per_bank):
-                    r = i * per_bank + rr
-                    turned[unit, r] = bank[:, rr, :]
-                    for j, src in enumerate(unit):
-                        nc.tensor.transpose(
-                            bank[:, rr, j * T_TILE : (j + 1) * T_TILE], dealt[src][:, r, :], ident[:]
-                        )
-
-        def columns(unit):
-            h, tt = groups[unit[0]]
-            return h, tt * T_TILE, T_TILE * len(unit)
-
-        def gelu(unit, rows_per_store):
-            h, t0, width = columns(unit)
-            result[unit] = sb.tile([P, PACK, width], F32, name="result%d" % unit[0])
-            rows = out_0[N_HALF * h : N_HALF * (h + 1), t0 : t0 + width].rearrange("(p r) t -> p r t", r=PACK)
+        def gelu_low(tt0):
+            low_out[tt0] = sb.tile([P, PACK, 2 * T_TILE], F32, name="low_out%d" % tt0)
             for r in range(PACK):
                 nc.scalar.activation(
-                    out=result[unit][:, r, :],
-                    in_=turned[unit, r],
+                    out=low_out[tt0][:, r, :],
+                    in_=turned[tt0, r],
                     func=ACT.Gelu_apprx_tanh,
-                    bias=bias[:, h, r : r + 1],
+                    bias=bias[:, LOW, r : r + 1],
                 )
-                if (r + 1) % rows_per_store == 0:
-                    done = slice(r + 1 - rows_per_store, r + 1)
-                    nc.sync.dma_start(out=rows[:, done, :], in_=result[unit][:, done, :])
+                if r % 2 == 1:
+                    nc.sync.dma_start(
+                        out=out_rows[LOW, :, r - 1 : r + 1, t_cols(tt0, tt0 + 2)],
+                        in_=low_out[tt0][:, r - 1 : r + 1, :],
+                    )
 
-        def round_result(unit):
-            h, t0, width = columns(unit)
-            narrow[unit] = sb.tile([P, PACK * width], BF16, name="narrow%d" % unit[0], align_bytes=64)
-            nc.vector.tensor_copy(out=grouped(narrow[unit][:]), in_=by_pairs(result[unit][:]))
+        def gelu_high(r, pieces):
+            step = T_TILES // pieces
+            for tt0 in range(0, T_TILES, step):
+                nc.scalar.activation(
+                    out=high_out[:, r, t_cols(tt0, tt0 + step)],
+                    in_=high_sum[r][:, t_cols(tt0, tt0 + step)],
+                    func=ACT.Gelu_apprx_tanh,
+                    bias=bias[:, HIGH, r : r + 1],
+                )
+            nc.sync.dma_start(out=out_rows[HIGH, :, r, :], in_=high_out[:, r, :])
 
-        def quantize_result(unit):
-            h, t0, width = columns(unit)
+        def round_out(h, tt0, tt1, on_vector):
+            src = low_out[tt0][:] if h == LOW else high_out[:, :, t_cols(tt0, tt1)]
+            name = "narrow%d_%d" % (h, tt0)
+            narrow[h, tt0] = sb.tile([P, PACK * (tt1 - tt0) * T_TILE], BF16, name=name, align_bytes=64)
+            if on_vector:
+                nc.vector.tensor_copy(out=as_words(narrow[h, tt0][:]), in_=as_rows(src))
+            else:
+                nc.scalar.copy(out=as_words(narrow[h, tt0][:]), in_=as_rows(src))
+
+        def quantize_out(h, tt0, tt1):
             nc.vector.quantize_mx(
-                out=out_codes[h][:, t0 : t0 + width].bitcast(FP8X4),
-                scales=out_scales[:, T * h + t0 : T * h + t0 + width],
-                in_=narrow[unit][:],
+                out=out_codes[h][:, t_cols(tt0, tt1)].bitcast(FP8X4),
+                scales=out_plane[:, t_cols(T_TILES * h + tt0, T_TILES * h + tt1)],
+                in_=narrow[h, tt0][:],
             )
 
-        code_rows = out_1.rearrange("a p t i -> a p (t i)").bitcast(I32)
+        def store_codes(h, tt0, tt1):
+            nc.sync.dma_start(
+                out=code_rows[h, :, t_cols(tt0, tt1)], in_=out_codes[h][:, t_cols(tt0, tt1)].bitcast(I32)
+            )
 
-        def store_codes(h, t0, t1):
-            nc.sync.dma_start(out=code_rows[h, :, t0:t1], in_=out_codes[h][:, t0:t1].bitcast(I32))
+        finish_low(0)
+        sort_low(0, True)
+        for tt in range(1, T_TILES - 1):
+            finish_low(tt)
+            sort_low(tt, False)
+        for a in (LAST - 1, LAST):
+            deal_w8(a)
+        deal_w4(LAST)
+        finish_low(T_TILES - 1)
+        sort_low(T_TILES - 1, True)
 
-        finish(0)
-        deal(0, True)
-        finish(1)
-        deal(1, False)
-        finish(2)
-        deal_w8(2)
-        deal_w8(3)
-        deal(2, False)
-        finish(3)
-        deal_w4(3)
-        deal(3, True)
-        turn((0, 1,), [0, 1])
-        gelu((0, 1,), 2)
-        finish_dealt(0)
-        turn((2, 3,), [2, 3])
-        gelu_dealt(0, 1)
-        gelu((2, 3,), 2)
-        finish_dealt(1)
-        finish_dealt(2)
-        finish_dealt(3)
-        round_result((0, 1,))
-        gelu_dealt(1, 1)
-        quantize_result((0, 1,))
-        round_result((2, 3,))
-        gelu_dealt(2, 1)
-        quantize_result((2, 3,))
-        store_codes(0, 0 * T_TILE, 4 * T_TILE)
-        gelu_dealt(3, 2)
-        round_high(0, 2, True)
-        round_high(3, 4, False)
-        round_high(2, 3, True)
-        quantize_high(0, 2)
-        store_codes(1, 0 * T_TILE, 2 * T_TILE)
-        quantize_high(2, 3)
-        quantize_high(3, 4)
-        store_codes(1, 2 * T_TILE, 4 * T_TILE)
-        scale_rows = out_2.bitcast(I32).rearrange("a (g r) t -> r g a t", r=QUADS)
-        planes = out_scales[:].bitcast(I32).rearrange("p (a t) -> p a t", a=HALVES)
-        for r in range(QUADS):
-            queue = nc.sync if r % 2 == 0 else nc.scalar
-            queue.dma_start(out=scale_rows[r], in_=planes[r:P:32, :, :])
+        turn_low(0)
+        gelu_low(0)
+        finish_high(0)
+        turn_low(2)
+        gelu_high(0, 1)
+        gelu_low(2)
+        for r in range(1, PACK):
+            finish_high(r)
+        for r in range(1, PACK - 1):
+            gelu_high(r, 1)
+        for tt0 in (0, 2):
+            round_out(LOW, tt0, tt0 + 2, True)
+            quantize_out(LOW, tt0, tt0 + 2)
+        store_codes(LOW, 0, T_TILES)
+
+        gelu_high(PACK - 1, 2)
+        round_out(HIGH, 0, 2, True)
+        round_out(HIGH, 3, 4, False)
+        round_out(HIGH, 2, 3, True)
+        quantize_out(HIGH, 0, 2)
+        store_codes(HIGH, 0, 2)
+        quantize_out(HIGH, 2, 3)
+        quantize_out(HIGH, 3, 4)
+        store_codes(HIGH, 2, T_TILES)
+
+        scale_rows = out_2.bitcast(I32).rearrange("h (g s) t -> s g h t", s=SCALE_ROWS)
+        plane_words = out_plane[:].bitcast(I32).rearrange("p (h t) -> p h t", h=M // N_HALF)
+        for s in range(SCALE_ROWS):
+            queue = nc.sync if s % 2 == 0 else nc.scalar
+            queue.dma_start(out=scale_rows[s], in_=plane_words[s:P:QUADRANT, :, :])

from contextlib import ExitStack

import concourse.mybir as mybir
from concourse.masks import make_identity

K, M, T = 2048, 1024, 512
FLOPS = 2 * 2 * K * M * T

F32 = mybir.dt.float32
BF16 = mybir.dt.bfloat16
I32 = mybir.dt.int32
U32 = mybir.dt.uint32
U8 = mybir.dt.uint8
FP8X4 = mybir.dt.float8_e4m3fn_x4
FP4X4 = mybir.dt.float4_e2m1fn_x4
ACT = mybir.ActivationFunctionType
ALU = mybir.AluOpType

P = 128
PACK = 4
K_PASS = P * PACK
PASSES = K // K_PASS
LAST = PASSES - 1
T_TILE = 128
T_TILES = T // T_TILE
N_HALF = 512
LOW, HIGH = 0, 1
QUADRANT = 32
SCALE_ROWS = 4
PASS_PAIR = 2
RUN = 2
LINE_WORDS = 4


def tile_mix_feat_fm_crelupl_gelu_kernel(
    tc, x, w4_words, w4_scales, w8_words, w8_scales, b, out_0, out_1, out_2
):
    nc = tc.nc

    with ExitStack() as ctx:
        sb = ctx.enter_context(tc.tile_pool(name="sb", bufs=1))
        psum = ctx.enter_context(tc.psum_pool(name="psum", bufs=1))
        ctx.enter_context(tc.manual_schedule())

        w4_planes = []
        for i in range(PASSES // PASS_PAIR):
            w4_planes.append(sb.tile([P, PASS_PAIR, M], U8, name="w4_planes%d" % i, align_bytes=64))
        w8_planes = sb.tile([P, M], U8, name="w8_planes", align_bytes=64)
        nc.vector.memset(w4_planes[0][:].bitcast(I32), 0)
        nc.vector.memset(w8_planes[:].bitcast(I32), 0)
        nc.vector.memset(w4_planes[1][:].bitcast(I32), 0)
        ident = sb.tile([P, P], F32, name="ident")
        make_identity(nc, ident[:])

        preload = sb.tile([P, 1], F32, name="preload")
        nc.scalar.activation(out=preload[:], in_=ident[:, 0:1], func=ACT.Gelu_apprx_tanh)

        w4_scale_rows = w4_scales.bitcast(I32).rearrange("a (g s) n -> s g a n", s=SCALE_ROWS)
        w8_scale_rows = w8_scales.bitcast(I32)
        w4_rows = w4_words.bitcast(I32).rearrange("a p n -> p a n")
        w8_rows = w8_words.rearrange("a p n i -> p a (n i)").bitcast(I32)
        raw = {}
        w4 = {}
        w8 = {}

        def load_x(a):
            raw[a] = sb.tile([P, PACK, T], F32, name="raw%d" % a)
            rows = x[a * K_PASS : (a + 1) * K_PASS, :]
            nc.sync.dma_start(out=raw[a][:], in_=rows.rearrange("(p j) t -> p j t", j=PACK))

        def load_w4(a, halves):
            n0, n1 = N_HALF * halves[0], N_HALF * (halves[-1] + 1)
            words = sb.tile([P, 1, 2 * (n1 - n0)], U8, name="w4_%d_%d" % (a, halves[0]), align_bytes=64)
            nc.sync.dma_start(out=words[:].bitcast(I32), in_=w4_rows[:, a : a + 1, n0 // 2 : n1 // 2])
            for h in halves:
                w4[a, h] = words[:, 0, 2 * (N_HALF * h - n0) : 2 * (N_HALF * (h + 1) - n0)]

        def load_w8(passes, halves):
            n0, n1 = N_HALF * halves[0], N_HALF * (halves[-1] + 1)
            name = "w8_%d_%d" % (passes[0], halves[0])
            words = sb.tile([P, len(passes), n1 - n0], U32, name=name, align_bytes=64)
            nc.sync.dma_start(out=words[:].bitcast(I32), in_=w8_rows[:, passes[0] : passes[-1] + 1, n0:n1])
            for i, a in enumerate(passes):
                for h in halves:
                    w8[a, h] = words[:, i, N_HALF * h - n0 : N_HALF * (h + 1) - n0]

        def load_w4_planes(i):
            for s in range(SCALE_ROWS):
                nc.sync.dma_start(
                    out=w4_planes[i][:].bitcast(I32)[s:P:QUADRANT, :, :],
                    in_=w4_scale_rows[s, :, PASS_PAIR * i : PASS_PAIR * (i + 1), :],
                )

        def load_w8_planes():
            for g in range(P // QUADRANT):
                nc.sync.dma_start(
                    out=w8_planes[:].bitcast(I32)[QUADRANT * g : QUADRANT * g + SCALE_ROWS * PASSES, :],
                    in_=w8_scale_rows[:, SCALE_ROWS * g : SCALE_ROWS * (g + 1), :],
                )

        load_x(0)
        load_w4_planes(0)
        load_w4(0, [LOW, HIGH])
        load_w8([0], [LOW, HIGH])
        load_w8_planes()
        load_x(1)
        load_w4(1, [LOW, HIGH])
        load_w8([1], [LOW, HIGH])
        load_x(2)
        load_w4_planes(1)
        load_w4(2, [LOW, HIGH])
        load_x(LAST)
        load_w8([LAST - 1], [LOW])
        load_w4(LAST, [LOW])
        load_w8([LAST], [LOW])
        load_w8([LAST - 1, LAST], [HIGH])
        load_w4(LAST, [HIGH])
        bias = sb.tile([P, M // N_HALF, PACK], F32, name="bias")
        nc.sync.dma_start(out=bias[:], in_=b.rearrange("(h p r) -> p h r", h=M // N_HALF, r=PACK))

        def as_words(narrow_ap):
            return narrow_ap.rearrange("p (c i j) -> p c j i", i=RUN, j=PACK)

        def as_rows(wide_ap):
            return wide_ap.rearrange("p j (c i) -> p c j i", i=RUN)

        def t_cols(tt0, tt1):
            return slice(tt0 * T_TILE, tt1 * T_TILE)

        rounded = {}
        codes = {}
        planes = {}

        def positive_part(a, tt, on_vector):
            dst = sb.tile([P, PACK * T_TILE], BF16, name="xa%d_%d" % (a, tt), align_bytes=64)
            src = as_rows(raw[a][:, :, t_cols(tt, tt + 1)])
            if on_vector:
                nc.vector.tensor_scalar(out=as_words(dst[:]), in0=src, scalar1=0.0, scalar2=None, op0=ALU.max)
            else:
                nc.scalar.activation(out=as_words(dst[:]), in_=src, func=ACT.Relu)
            rounded["a", a, tt] = dst

        def negative_part(a, tt):
            dst = sb.tile([P, PACK * T_TILE], BF16, name="xb%d_%d" % (a, tt), align_bytes=64)
            src = as_rows(raw[a][:, :, t_cols(tt, tt + 1)])
            nc.scalar.activation(out=as_words(dst[:]), in_=src, func=ACT.Relu, scale=-1.0)
            rounded["b", a, tt] = dst

        def quantize_x(part, a, tt):
            if (part, a) not in codes:
                codes[part, a] = sb.tile([P, T], U32, name="codes_%s%d" % (part, a), align_bytes=64)
                planes[part, a] = sb.tile([P, T], U8, name="plane_%s%d" % (part, a), align_bytes=64)
            nc.vector.quantize_mx(
                out=codes[part, a][:, t_cols(tt, tt + 1)].bitcast(FP8X4),
                scales=planes[part, a][:, t_cols(tt, tt + 1)],
                in_=rounded[part, a, tt][:],
            )

        low_sum = []
        for tt in range(T_TILES):
            low_sum.append(psum.tile([P, N_HALF], F32, name="low_sum%d" % tt, tag="bank%d" % tt))
        high_sum = []
        for r in range(PACK):
            high_sum.append(psum.tile([P, T], F32, name="high_sum%d" % r, tag="bank%d" % (T_TILES + r)))

        def low_w4(a, tt):
            nc.tensor.matmul_mx(
                out=low_sum[tt][:],
                lhsT=codes["a", a][:, t_cols(tt, tt + 1)].bitcast(FP8X4),
                lhsT_scale=planes["a", a][:, t_cols(tt, tt + 1)],
                rhs=w4[a, LOW].bitcast(FP4X4),
                rhs_scale=w4_planes[a // PASS_PAIR][:, a % PASS_PAIR, 0:N_HALF],
                start=(a == 0),
                stop=False,
            )

        def low_w8(a, tt):
            nc.tensor.matmul_mx(
                out=low_sum[tt][:],
                lhsT=codes["b", a][:, t_cols(tt, tt + 1)].bitcast(FP8X4),
                lhsT_scale=planes["b", a][:, t_cols(tt, tt + 1)],
                rhs=w8[a, LOW].bitcast(FP8X4),
                rhs_scale=w8_planes[SCALE_ROWS * a : P, 0:N_HALF],
                start=False,
                stop=(a == LAST),
            )

        w4_dealt = {}
        w8_dealt = {}
        w4_plane_dealt = {}
        w8_planes_dealt = sb.tile([P, PACK, P], U8, name="w8_planes_dealt", align_bytes=64)

        def deal_w4(a):
            w4_dealt[a] = sb.tile([P, PACK, 2 * P], U8, name="w4_dealt%d" % a, align_bytes=64)
            nc.vector.tensor_copy(
                out=w4_dealt[a][:].rearrange("p r (m e) -> p r m e", e=2),
                in_=w4[a, HIGH].rearrange("p (m r e) -> p r m e", r=PACK, e=2),
            )

        def deal_w8(a):
            w8_dealt[a] = sb.tile([P, PACK, P], U32, name="w8_dealt%d" % a, align_bytes=64)
            nc.vector.tensor_copy(
                out=w8_dealt[a][:].bitcast(I32).rearrange("p r (c i) -> p c r i", i=LINE_WORDS),
                in_=w8[a, HIGH].bitcast(I32).rearrange("p (c i r) -> p c r i", i=LINE_WORDS, r=PACK),
            )

        def deal_w4_planes(i):
            pair = sb.tile([P, PASS_PAIR, PACK, P], U8, name="w4_planes_dealt%d" % i, align_bytes=64)
            nc.vector.tensor_copy(
                out=pair[:], in_=w4_planes[i][:, :, N_HALF:M].rearrange("p a (m r) -> p a r m", r=PACK)
            )
            for j in range(PASS_PAIR):
                w4_plane_dealt[PASS_PAIR * i + j] = pair[:, j, :, :]

        def deal_w8_planes():
            nc.vector.tensor_copy(
                out=w8_planes_dealt[:], in_=w8_planes[:, N_HALF:M].rearrange("p (m r) -> p r m", r=PACK)
            )

        def high_w4(a, r):
            nc.tensor.matmul_mx(
                out=high_sum[r][:],
                lhsT=w4_dealt[a][:, r, :].bitcast(FP4X4),
                lhsT_scale=w4_plane_dealt[a][:, r, :],
                rhs=codes["a", a][:].bitcast(FP8X4),
                rhs_scale=planes["a", a][:],
                start=(a == 0),
                stop=(a == LAST),
            )

        def high_w8(a, r):
            nc.tensor.matmul_mx(
                out=high_sum[r][:],
                lhsT=w8_dealt[a][:, r, :].bitcast(FP8X4),
                lhsT_scale=w8_planes_dealt[SCALE_ROWS * a : P, r, :],
                rhs=codes["b", a][:].bitcast(FP8X4),
                rhs_scale=planes["b", a][:],
                start=False,
                stop=False,
            )

        for a in range(LAST):
            positive_part(a, T_TILES - 1, False)
            for tt in range(T_TILES):
                negative_part(a, tt)
            positive_part(a, 0, True)
            positive_part(a, 1, True)
            quantize_x("a", a, 0)
            positive_part(a, 2, True)
            for tt in range(1, T_TILES):
                quantize_x("a", a, tt)
            if a % PASS_PAIR == 0:
                deal_w4_planes(a // PASS_PAIR)
            deal_w4(a)
            for tt in range(T_TILES):
                quantize_x("b", a, tt)
            if a == 0:
                deal_w8_planes()
            for tt in range(T_TILES):
                low_w4(a, tt)
            for r in range(PACK):
                high_w4(a, r)
            if a < LAST - 1:
                deal_w8(a)
            for tt in range(T_TILES):
                low_w8(a, tt)
            if a < LAST - 1:
                for r in range(PACK):
                    high_w8(a, r)

        for tt in range(T_TILES):
            negative_part(LAST, tt)
        positive_part(LAST, 0, True)
        for tt in range(T_TILES):
            if tt + 1 < T_TILES:
                positive_part(LAST, tt + 1, True)
            quantize_x("a", LAST, tt)
            quantize_x("b", LAST, tt)

        out_plane = sb.tile([P, M // N_HALF * T], U8, name="out_plane", align_bytes=64)
        out_codes = []
        for h in (LOW, HIGH):
            out_codes.append(sb.tile([P, T], U32, name="out_codes%d" % h, align_bytes=64))
        high_out = sb.tile([P, PACK, T], F32, name="high_out")
        out_rows = out_0.rearrange("(h p r) t -> h p r t", h=M // N_HALF, r=PACK)
        code_rows = out_1.rearrange("a p t i -> a p (t i)").bitcast(I32)
        sorted_sum = {}
        turned = {}
        low_out = {}
        narrow = {}

        def finish_low(tt):
            low_w4(LAST, tt)
            low_w8(LAST, tt)

        def finish_high(r):
            high_w8(LAST - 1, r)
            high_w8(LAST, r)
            high_w4(LAST, r)

        def sort_low(tt, on_vector):
            sorted_sum[tt] = sb.tile([P, PACK, P], F32, name="sorted_sum%d" % tt)
            src = low_sum[tt][:].rearrange("t (p r) -> t r p", r=PACK)
            if on_vector:
                nc.vector.tensor_copy(out=sorted_sum[tt][:], in_=src)
            else:
                nc.scalar.copy(out=sorted_sum[tt][:], in_=src)

        def turn_low(tt0):
            for i in range(2):
                name = "turned%d" % (tt0 + i)
                bank = psum.tile([P, 2, 2 * T_TILE], F32, name=name, tag="bank%d" % (tt0 + i))
                for rr in range(2):
                    turned[tt0, 2 * i + rr] = bank[:, rr, :]
                    for j in range(2):
                        src = sorted_sum[tt0 + j][:, 2 * i + rr, :]
                        nc.tensor.transpose(bank[:, rr, t_cols(j, j + 1)], src, ident[:])

        def gelu_low(tt0):
            low_out[tt0] = sb.tile([P, PACK, 2 * T_TILE], F32, name="low_out%d" % tt0)
            for r in range(PACK):
                nc.scalar.activation(
                    out=low_out[tt0][:, r, :],
                    in_=turned[tt0, r],
                    func=ACT.Gelu_apprx_tanh,
                    bias=bias[:, LOW, r : r + 1],
                )
                if r % 2 == 1:
                    nc.sync.dma_start(
                        out=out_rows[LOW, :, r - 1 : r + 1, t_cols(tt0, tt0 + 2)],
                        in_=low_out[tt0][:, r - 1 : r + 1, :],
                    )

        def gelu_high(r, pieces):
            step = T_TILES // pieces
            for tt0 in range(0, T_TILES, step):
                nc.scalar.activation(
                    out=high_out[:, r, t_cols(tt0, tt0 + step)],
                    in_=high_sum[r][:, t_cols(tt0, tt0 + step)],
                    func=ACT.Gelu_apprx_tanh,
                    bias=bias[:, HIGH, r : r + 1],
                )
            nc.sync.dma_start(out=out_rows[HIGH, :, r, :], in_=high_out[:, r, :])

        def round_out(h, tt0, tt1, on_vector):
            src = low_out[tt0][:] if h == LOW else high_out[:, :, t_cols(tt0, tt1)]
            name = "narrow%d_%d" % (h, tt0)
            narrow[h, tt0] = sb.tile([P, PACK * (tt1 - tt0) * T_TILE], BF16, name=name, align_bytes=64)
            if on_vector:
                nc.vector.tensor_copy(out=as_words(narrow[h, tt0][:]), in_=as_rows(src))
            else:
                nc.scalar.copy(out=as_words(narrow[h, tt0][:]), in_=as_rows(src))

        def quantize_out(h, tt0, tt1):
            nc.vector.quantize_mx(
                out=out_codes[h][:, t_cols(tt0, tt1)].bitcast(FP8X4),
                scales=out_plane[:, t_cols(T_TILES * h + tt0, T_TILES * h + tt1)],
                in_=narrow[h, tt0][:],
            )

        def store_codes(h, tt0, tt1):
            nc.sync.dma_start(
                out=code_rows[h, :, t_cols(tt0, tt1)], in_=out_codes[h][:, t_cols(tt0, tt1)].bitcast(I32)
            )

        finish_low(0)
        sort_low(0, True)
        for tt in range(1, T_TILES - 1):
            finish_low(tt)
            sort_low(tt, False)
        for a in (LAST - 1, LAST):
            deal_w8(a)
        deal_w4(LAST)
        finish_low(T_TILES - 1)
        sort_low(T_TILES - 1, True)

        turn_low(0)
        gelu_low(0)
        finish_high(0)
        turn_low(2)
        gelu_high(0, 1)
        gelu_low(2)
        for r in range(1, PACK):
            finish_high(r)
        for r in range(1, PACK - 1):
            gelu_high(r, 1)
        for tt0 in (0, 2):
            round_out(LOW, tt0, tt0 + 2, True)
            quantize_out(LOW, tt0, tt0 + 2)
        store_codes(LOW, 0, T_TILES)

        gelu_high(PACK - 1, 2)
        round_out(HIGH, 0, 2, True)
        round_out(HIGH, 3, 4, False)
        round_out(HIGH, 2, 3, True)
        quantize_out(HIGH, 0, 2)
        store_codes(HIGH, 0, 2)
        quantize_out(HIGH, 2, 3)
        quantize_out(HIGH, 3, 4)
        store_codes(HIGH, 2, T_TILES)

        scale_rows = out_2.bitcast(I32).rearrange("h (g s) t -> s g h t", s=SCALE_ROWS)
        plane_words = out_plane[:].bitcast(I32).rearrange("p (h t) -> p h t", h=M // N_HALF)
        for s in range(SCALE_ROWS):
            queue = nc.sync if s % 2 == 0 else nc.scalar
            queue.dma_start(out=scale_rows[s], in_=plane_words[s:P:QUADRANT, :, :])
